import numpy as np, ml_dtypes
CORES = [16,18,20,22]
N = 4
import mx_ref
BF = ml_dtypes.bfloat16
def cols(t, e):
    v = np.concatenate([t.reshape(128, -1, 4), np.zeros((128, 1, 4), BF)], axis=1)
    return np.ascontiguousarray(v[:, e]).reshape(128, -1)
def cut(t, i, w=512):
    return t[:, w * i:w * i + w]
def tile(rs):
    return np.stack(rs, axis=2).reshape(128, -1).astype(BF)
def pick(q, e):
    c = np.concatenate([q[0].reshape(128, -1, 4), np.zeros((128, 1, 4), np.uint8)], axis=1); s = np.concatenate([q[1], np.ones((16, 1), np.uint8)], axis=1)
    return (np.ascontiguousarray(c[:, e].reshape(128, -1)), np.ascontiguousarray(s[:, e]))
def join(*qs):
    return (np.concatenate([q[0] for q in qs], axis=1), np.concatenate([q[1] for q in qs], axis=1))
def put(q, e, v):
    c, s = q[0].reshape(128, -1, 4).copy(), q[1].copy(); c[:, e] = v[0].reshape(128, -1, 4); s[:, e] = v[1]
    return (c.reshape(128, -1), s)
def pk(c, s):
    return (np.ascontiguousarray(c), mx_ref.live(s))
def emit(q):
    return q[0], q[1]
def decode(q):
    o = []
    for b in range(4):
        e = np.zeros((128, 128, 4), np.float32); e[np.arange(128), np.arange(128), b] = 1
        o.append(mx_ref.matmul(mx_ref.quantize(e.reshape(128, 512).astype(BF)), q))
    return np.stack(o, axis=2).reshape(128, -1)
def f(rng, *shape):
    return mx_ref.flush((rng.standard_normal(shape, dtype=np.float32) * np.exp2(rng.integers(-2, 3, shape[:-1] + (1,)))).astype(BF))
def wide(rng, *shape, cols=0):
    v = rng.standard_normal(shape, dtype=np.float32) * np.exp2(rng.integers(-12, 13, shape)).astype(np.float32)
    if cols: v *= np.repeat(np.exp2(rng.integers(-cols, cols + 1, shape[:-2] + (1, shape[-1] // 4))) * (rng.random(shape[:-2] + (1, shape[-1] // 4)) > 0.0625), 4, axis=-1).astype(np.float32)
    return mx_ref.flush(v.astype(BF))
T, A, KM, CAPP, FA = 192, 32, 64, 32, 2
def big(t):
    t = np.array(t)
    t[np.abs(t.astype(np.float32)) < np.float32(2.0 ** -16)] = 0
    return t
def plain(rng):
    x = np.concatenate([f(rng, N, 128, 4 * A), f(rng, N, 128, 4 * (T - A))], axis=2)
    return {"x": big(x), "w": f(rng, N, 128, 2048), "v": f(rng, N, 128, 512)}
def pull(rng, x, at, who, n=8, bare=False):
    x = np.array(x).reshape(N, 128, T, 4)
    x[:, :n * len(at)] = 0
    for i, (q, a) in enumerate(at):
        if bare: x[q, :, a] = 0
        x[q, n * i:n * i + n, a] = (32 * (1 + rng.random((n, 4)))).astype(np.float32).astype(BF)
        r, j = np.nonzero(who == i)
        x[r, n * i:n * i + n, j] = (8 * (1 + rng.random((len(r), n, 4)))).astype(np.float32).astype(BF)
    return x.reshape(N, 128, 4 * T)
def setup_inputs(rng):
    return plain(rng)
def setup_inputs_crowd(rng):
    d, who = plain(rng), np.full((N, T), -1)
    z, q = int(rng.integers(1, N)), rng.permutation(N)[:2]
    for r in range(N):
        e = A + rng.permutation(T - A)[:KM * 5 // 6 + FA]
        who[r, e] = 0
        who[r, e[:FA]] = 1
    who[z, A:] = rng.integers(0, 2, T - A)
    d["x"] = pull(rng, d["x"], [(int(q[i]), int(rng.integers(0, A))) for i in range(2)], who)
    return d
def setup_inputs_full(rng):
    d, who, o = plain(rng), np.full((N, T), -1), rng.permutation(N)
    g = FA * A // CAPP
    e = np.tile(rng.permutation(A), FA).reshape(g, CAPP)
    for i, s in enumerate(np.sort(o[1:g + 1])):
        who[s, A:A + CAPP] = rng.permutation(e[i])
        who[s, A + CAPP:A + CAPP + 4] = e[-1, -1]
    d["x"] = pull(rng, d["x"], [(int(o[0]), a) for a in range(A)], who, 2, True)
    return d
def setup_inputs_ties(rng):
    d = plain(rng)
    x = np.array(d["x"])
    part = np.arange(128) // 8
    m = rng.permutation(N * A) % (N * A // 4)
    k = cols(np.concatenate([x[q][:, :4 * A] for q in range(N)], axis=1), rng.permutation(N * A)[m])
    k = np.abs(k.astype(np.float32)) * np.repeat(np.where(part[:, None] == m % 16, 2.0 ** -8, 1.0), 4, axis=1)
    k = big(k.astype(np.float32).astype(BF))
    for r in range(N):
        g = rng.permutation(np.arange(T - A) // 7)
        u = cols(np.ascontiguousarray(x[r][:, 4 * A:]), g)
        if r == 0:
            on = part[:, None] == (m[0] + 1 + g % 15) % 16
            u = (-np.abs(u.astype(np.float32)) * np.repeat(on, 4, axis=1)).astype(BF)
        if r == 1:
            u = np.abs(u.astype(np.float32)).reshape(128, T - A, 4)
            o = np.append(0, 1 + rng.permutation(T - A - 1)[KM // 2:])
            u[:, o[::2]] = -0.0
            u[:, o[1::2]] = 0.0
            u = u.astype(BF).reshape(128, -1)
        x[r][:, 4 * A:] = u
        x[r][:, :4 * A] = cut(k, r, 4 * A)
    d["x"] = x
    return d
def setup_inputs_own(rng):
    d = plain(rng)
    x = np.array(d["x"])
    x[:, :, 2 * A:4 * A] = -x[:, :, :2 * A]
    x[(np.arange(128) // (128 // N))[None, :] != np.arange(N)[:, None]] = 0
    d["x"] = x
    return d
def setup_inputs_spread(rng):
    return {**plain(rng), "x": big(wide(rng, N, 128, 4 * T, cols=4))}
def check_inputs(d):
    b = []
    for k in ("x", "w", "v"):
        t = np.abs(d[k].astype(np.float32))
        if not (np.isfinite(t).all() and ((t == 0) | (t >= 2.0 ** -30) & (t <= 2.0 ** 30)).all()): b.append("a value of " + k)
    return b
def choose(x):
    k = np.concatenate([x[q][:, :4 * A] for q in range(N)], axis=1)
    k = [mx_ref.quantize(np.ascontiguousarray(cut(k, i))) for i in range(N * A // 128)]
    goal, took, have = np.full((N, T), -1), np.full((N, A, FA), -1), np.zeros((N, A), int)
    for s in range(N):
        u = mx_ref.quantize(np.ascontiguousarray(x[s][:, 4 * A:]))
        z = np.concatenate([mx_ref.matmul(t, u) for t in k]) + np.float32(0.0)
        best = np.argmax(z, axis=0)
        offers = np.sort(np.argsort(-z.max(axis=0), kind="stable")[:KM])
        stand = np.zeros(N, int)
        for j in offers:
            q, a = best[j] // A, best[j] % A
            if stand[q] == CAPP: continue
            stand[q] += 1
            if have[q, a] == FA: continue
            took[q, a, have[q, a]] = s * T + A + j
            have[q, a] += 1
            goal[s, A + j] = q * T + a
    return goal, took
def reference(x, w, v):
    goal, took = choose(x)
    c = [mx_ref.quantize(np.ascontiguousarray(x[r])) for r in range(N)]
    d = np.concatenate([decode(c[r]).reshape(128, T, 4) for r in range(N)], axis=1)
    h = []
    for q in range(N):
        m = d[:, q * T:q * T + A].copy()
        for t in range(FA):
            a = np.flatnonzero(took[q, :, t] >= 0)
            m[:, a] = m[:, a] + d[:, took[q, a, t]]
        new = mx_ref.quantize(np.ascontiguousarray((m * np.float32(0.5)).reshape(128, -1).astype(BF)))
        a = np.flatnonzero(took[q, :, 0] >= 0)
        k = put(c[q], a, pick(new, a))
        rs = [np.maximum(mx_ref.matmul(mx_ref.quantize(np.ascontiguousarray(cut(w[q], i))), k), np.float32(0.0)) * np.float32(0.0625) for i in range(4)]
        h.append(mx_ref.quantize(np.ascontiguousarray(tile(rs))))
    every = join(*h)
    oc, osc = np.zeros((N, 128, 4 * T), np.uint8), np.zeros((N, 16, T), np.uint8)
    mg, y = np.zeros((N, 1, T), np.float32), np.zeros((N, 128, T), np.float32)
    for s in range(N):
        g = pick(every, np.where(goal[s] >= 0, goal[s], s * T + np.arange(T)))
        oc[s], osc[s] = emit(g)
        mg[s, 0] = goal[s]
        y[s] = mx_ref.matmul(mx_ref.quantize(np.ascontiguousarray(v[s])), g)
    return {"oc": oc, "osc": osc, "mg": mg, "y": y}

@@ -1,0 +1,501 @@
+from concourse.bass import DstId, RemoteDMATransfer
+from concourse.mybir import dt, AluOpType as Op, AxisListType, ActivationFunctionType as Act
+
+A = 32
+EPS, TINY = 1.25 * 2.0 ** -24, 2.0 ** -125
+F, B16, U16, CODE, PL = "float32", "bfloat16", "uint16", "float8_e4m3fn_x4", "uint8"
+
+SCRATCH = {}
+
+
+def _sb(dtype, **names):
+    for n, w in names.items():
+        SCRATCH[n] = ("sbuf", [128, w], dtype)
+
+
+def _mx(**names):
+    for n, w in names.items():
+        SCRATCH[n + "q"] = ("sbuf", [128, w], CODE)
+        SCRATCH[n + "p"] = ("sbuf", [128, w], PL)
+
+
+SCRATCH["psum"] = ("psum", [128, 4096], F)
+_sb(F, cst=16, th=8, kc=16, kx=16, colw=12, colm=12, mk=96, tri32=32, rst=160, mgt=320,
+    rmax=256, m5=8, a5=8, rep=224, mrow=224, jnk=256, tiny=64, kab=16,
+    ss=128, dw=10, crow=128, prior=160, adm=160, scn=160, admt=10, fin=12, fm=2, mgr=192, yo=192)
+_sb("int32", pidi=1, ui=1)
+_sb(B16, rowb=128, k16=256, kst=256, et=516, trt=640, s3t=512, zt=664, xz=512, xt=1152, wt=2048, vt=512,
+    cc=320, cj=320, ot=536, stt=512, s2t=512, tmt=688, mh=640, hot=768, hot10=20,
+    lst=16, nz=16, csum=8, ll=32, lc=24, lab=32, lu=16, lcm=2, lf=2, ctot=8)
+_sb(U16, colu=12, invu=8, off=4, gwu=10, cu=8, finu=12)
+_mx(e=512, tr=160, s3=128, a=128, x=288, k=192, w=512, v=128, ob=134, mm=136, st=128, s2=128, m2=128, tm=172,
+    sl=96, win=256, m=128, hm=128, hw=320, fo=192)
+
+SEMAPHORES = ["qv", "qs", "qt", "qg", "dxa", "dx", "dx2", "dw", "dv", "dz1", "dz2", "dz3", "dz4", "dkq", "dkp", "dzq", "dzp",
+              "an", "so", "li", "ct", "hm", "la", "lb", "dout"]
+_TINY = {n: 2 * i for i, n in enumerate(["cn", "gg", "gd", "gq", "gm", "gd16", "gd64", "yy", "lpv", "key", "hi", "yl8", "lo",
+                                         "thz", "thy", "thr", "sg1"])}
+
+
+def rank_program(g, core, T, topo):
+    s = T.rank_of(core)
+    if s is None:
+        return
+    others = [r for r in range(4) if r != s]
+    order = others + [s]
+    Q = {"v": g.vector, "s": g.scalar, "t": g.tensor, "g": g, "y": g.sync}
+    waited, lastw, readers, total = {q: {} for q in Q}, {}, {}, {}
+
+    def wait(q, toks):
+        need = {}
+        for n, val in toks:
+            need[n] = max(need.get(n, 0), val)
+        for n in sorted(need):
+            if waited[q].get(n, 0) < need[n]:
+                Q[q].wait_ge(T.sem[n], need[n])
+                waited[q][n] = need[n]
+
+    def run(q, fn, rd=(), wr=(), sem=None, free=()):
+        toks = []
+        for k in rd:
+            toks += lastw[k]
+        for k in wr:
+            if k not in free:
+                toks += lastw.get(k, []) + readers.get(k, [])
+        wait(q, toks)
+        n, inc = (sem, 16) if sem else ("q" + q, 1)
+        fn().then_inc(T.sem[n], inc)
+        total[n] = total.get(n, 0) + inc
+        tok = (n, total[n])
+        for k in rd:
+            readers.setdefault(k, []).append(tok)
+        for k in wr:
+            lastw[k] = [tok]
+            readers[k] = []
+
+    V, S, P = g.vector, g.scalar, g.tensor
+
+    def vts(out, in0, s1, s2, op0, op1=None, rd=(), wr=()):
+        if op1 is None:
+            run("v", lambda: V.tensor_scalar(out, in0, s1, None, op0), rd, wr)
+        else:
+            run("v", lambda: V.tensor_scalar(out, in0, s1, s2, op0, op1), rd, wr)
+
+    def vtt(out, a, b, op, rd=(), wr=()):
+        run("v", lambda: V.tensor_tensor(out, a, b, op), rd, wr)
+
+    def vcp(out, in_, rd=(), wr=()):
+        run("v", lambda: V.tensor_copy(out, in_), rd, wr)
+
+    def fill(ap, c, *wr):
+        run("v", lambda: V.memset(ap, c), (), wr)
+
+    def vred(out, in_, op, rd=(), wr=()):
+        run("v", lambda: V.tensor_reduce(out, in_, AxisListType.X, op), rd, wr)
+
+    def vscan(out, d0, d1, init, op0, op1, rd=(), wr=()):
+        run("v", lambda: V.tensor_tensor_scan(out, d0, d1, init, op0, op1), rd, wr)
+
+    def vtr(out, in_, rd=(), wr=()):
+        run("v", lambda: V.transpose(out, in_), rd, wr)
+
+    def act(out, in_, func, rd=(), wr=(), **kw):
+        run("s", lambda: S.activation(out, in_, func, **kw), rd, wr)
+
+    def iota(out, pattern, base, *wr, rd=(), cm=0):
+        run("g", lambda: g.iota(out, pattern, base, cm, allow_small_or_imprecise_dtypes=True), rd, wr)
+
+    def select(out, in_, pattern, op, fl, base, cm, rd, wr):
+        run("g", lambda: g.affine_select(out, in_, pattern, op, fl, base, cm), rd, wr)
+
+    def sync(out, in_, sem, rd=(), wr=()):
+        run("y", lambda: g.sync.dma_start(out, in_), rd, wr, sem=sem)
+
+    def quant(n, a, b, src, rd=(), wr=None):
+        run("v", lambda: V.quantize_mx(T[n + "q"][:, a:b], T[n + "p"][:, a:b], src), rd, wr or (n + "q", n + "p"))
+
+    def bank(i, a, b=None):
+        return T.psum[:, 512 * i:512 * i + a] if b is None else T.psum[:, 512 * i + a:512 * i + b]
+
+    def mm(i, n, ln, la, rn, ra, start=True, stop=True, rd=None, lrd=None):
+        b = "b%d" % i
+        run("t", lambda: P.matmul_mx(bank(i, n), T[ln + "q"][:, la:la + 128], T[ln + "p"][:, la:la + 128],
+                                     T[rn + "q"][:, ra:ra + n], T[rn + "p"][:, ra:ra + n], start, stop),
+            (lrd or (ln + "q", ln + "p")) + (rd or (rn + "q", rn + "p")), (b,), free=() if start else (b,))
+
+    def pickq(dn, c, d, sn, lo, hi, off, rd, wr):
+        run("v", lambda: V.tensor_copy(T[dn + "q"][:, c:d].bitcast(dt.uint32),
+                                       T[sn + "q"][:, lo:hi].bitcast(dt.uint32).indirect(off)), rd, wr)
+
+    def pickp(dn, c, d, sn, lo, hi, off, rd, wr):
+        run("s", lambda: S.activation(T[dn + "p"][:, c:d], T[sn + "p"][:, lo:hi].indirect(off), Act.Copy), rd, wr)
+
+    def tn(n, i=None):
+        c = _TINY[n]
+        return T.tiny[:, c:c + 2] if i is None else T.tiny[:, c + i:c + i + 1]
+
+    def addr(r):
+        rid, pid, _ = topo.addr(T.cores[r])
+        return DstId(rid=rid, pnc=pid)
+
+    def msk(es):
+        return sum(1 << e for e in es)
+
+    lsum = {"la": 0, "lb": 0}
+
+    def bcast(src, dst, sem, local, rd):
+        eng = topo.engines(core, T.cores[others[0]])
+        wait("g", [t for k in rd for t in lastw[k]])
+        g.remote_dma_fused([RemoteDMATransfer(dst_ids=[addr(r) for r in others], dma_engine_mask=msk(eng),
+                                              remote_sem=T.sem[sem], srcs=[src], dsts=[dst] * len(others))],
+                           local_sem=T.sem[local])
+        lsum[local] += len(eng)
+
+    def scatter(srcs, dst, dests, sem, local, rd, first=0):
+        wait("g", [t for k in rd for t in lastw[k]])
+        tr = []
+        for i, (r, src) in enumerate(zip(dests, srcs)):
+            eng = topo.engines(core, T.cores[r])
+            j = 4 * ((first + i) % 4)
+            tr.append(RemoteDMATransfer(dst_ids=[addr(r)], dma_engine_mask=msk(eng[j:j + 4]), remote_sem=T.sem[sem],
+                                        src=src, dst=dst))
+        g.remote_dma_fused(tr, local_sem=T.sem[local])
+        lsum[local] += 4 * len(tr)
+
+    u8 = dt.uint8
+
+    def cs(j):
+        return T.cst[:, j:j + 1]
+
+    D1, D2 = 64, 600
+    Z = T.zt[:, D1:D2]
+
+    sync(T.xz[:, 0:128], T.x[:, 0:128], "dxa", (), ("xza",))
+    run("s", lambda: S.dma_start(T.xt[:, 0:768], T.x[:, :]), (), ("xt",), sem="dx")
+    sync(T.xt[:, 768:1152], T.x[:, 128:512], "dx2", (), ("xt2",))
+
+    run("g", lambda: g.iota(T.pidi[:], [[0, 1]], 0, 1), (), ("pidi",))
+    iota(cs(0), [[0, 1]], 0, "c0", cm=1)
+    iota(T.rowb[:], [[1, 128]], 0, "rowb")
+
+    fill(T.xz[:, 128:512], 0.0, "xzz")
+    run("v", lambda: V.tensor_scalar(T.ui[:], T.pidi[:], 31, None, Op.bitwise_and), ("pidi",), ("ui",))
+    fill(Z, 0.0, "zt")
+    vcp(cs(2), T.ui[:], ("ui",), ("c2",))
+    fill(T.ll[:], 0.0, "ll")
+    quant("a", 0, 128, T.xz[:], ("xza", "xzz"))
+    at1 = 64 + A * s
+    bcast(T.aq[:, 0:A].bitcast(u8), T.kq[:, at1:at1 + A].bitcast(u8), "an", "la", ("aq",))
+    bcast(T.ap[:, 0:A], T.kp[:, at1:at1 + A], "an", "la", ("ap",))
+    lastw["kq"] = lastw["kp"] = [("an", 96)]
+    iota(T.th[:, 0:7], [[0, 7]], 1, "th")
+    select(T.th[:, 0:7], T.th[:, 0:7], [[-16, 7]], Op.is_ge, 0.0, -16, 1, ("th",), ("th",))
+    sync(T.kq[:, at1:at1 + A].bitcast(u8), T.aq[:, 0:A].bitcast(u8), "dkq", ("aq",), ("kqo",))
+    sync(T.kp[:, at1:at1 + A], T.ap[:, 0:A], "dkp", ("ap",), ("kpo",))
+    wait("y", [("la", lsum["la"])])
+    sync(T.ot[:, 0:536], Z, "dz4", ("zt",), ("otA", "otB", "otC", "otD", "otZ"))
+    sync(T.wt[:, :], T.w[:, :], "dw", (), ("wt",))
+    sync(T.winq[:, 96:128].bitcast(u8), T.aq[:, 96:128].bitcast(u8), "dzq", ("aq",), ("winqz",))
+    sync(T.winp[:, 96:128], T.ap[:, 96:128], "dzp", ("ap",), ("winpz",))
+    sync(T.tmt[:, 0:512], T.zt[:, D1:D1 + 512], "dz2", ("zt",), ("tm0",))
+    sync(T.tmt[:, 512:688], T.zt[:, D1:D1 + 176], "dz3", ("zt",), ("tm1",))
+    sync(T.mh[:, 128:512], T.zt[:, D1:D1 + 384], "dz1", ("zt",), ("mhz",))
+    sync(T.vt[:, :], T.v[:, :], "dv", (), ("vt",))
+    for i in range(2, 6):
+        lastw["tm%d" % i] = list(lastw["tm1"])
+
+    fill(T.et[:], 0.0, "et")
+    vts(T.et[:, 3:515:4], T.rowb[:], cs(0), 0.5, Op.is_equal, Op.mult, ("rowb", "c0"), ("et",))
+    quant("x", 0, 288, T.xt[:], ("xt", "xt2"))
+    for b in range(4):
+        quant("e", 128 * b, 128 * b + 128, T.et[:, 3 - b:515 - b], ("et",), ("eq%d" % b, "ep%d" % b))
+    act(T.mk[:], T.zt[:, D1:D1 + 96], Act.Copy, ("zt",), ("mk",), bias=1.0)
+    act(T.trt[:, 0:512], T.zt[:, D1:D1 + 512], Act.Copy, ("zt",), ("trA",))
+    act(T.trt[:, 512:640], T.zt[:, D1:D1 + 128], Act.Copy, ("zt",), ("trB", "trB2"))
+    act(T.tri32[:], T.rowb[:, 0:32], Act.Sign, ("rowb", "c2"), ("tri32",), scale=-1.0, bias=cs(2))
+    act(T.tri32[:], T.tri32[:], Act.Relu, ("tri32",), ("tri32",), scale=-1.0)
+    act(T.jnk[:, 128:135], T.th[:, 0:7], Act.Copy, ("th",), ("jnk1", "c3"), accum_out=cs(3))
+    act(cs(1), cs(3), Act.Identity, ("c3", "c0"), ("c1",), scale=-16.0, bias=cs(0))
+    act(cs(6), cs(3), Act.Copy, ("c3",), ("c6",), scale=16.0, bias=32.0)
+    act(cs(7), cs(3), Act.Copy, ("c3",), ("c7",), scale=16.0, bias=64.0)
+    act(cs(8), cs(1), Act.Copy, ("c1",), ("c8",), scale=-1.0)
+    act(cs(9), cs(3), Act.Copy, ("c3",), ("c9",), scale=-16.0, bias=-32.0)
+    select(T.mk[:], T.mk[:], [[32, 3], [0, 32]], Op.is_ge, 0.0, -96, 1, ("mk",), ("mk",))
+    tp = [[-1, 128]]
+    select(T.trt[:, 0:512:4], T.trt[:, 0:512:4], tp, Op.is_ge, -1.0, 0, 1, ("trA",), ("trA",))
+    select(T.trt[:, 0:512:4], T.trt[:, 0:512:4], tp, Op.not_equal, 32.0, 0, 1, ("trA",), ("trA",))
+    iota(T.trt[:, 512:640:4], [[0, 32]], -1, "trB2")
+    c = _TINY["yy"]
+    iota(T.tiny[:, c:c + 4], [[0, 4]], 0, "yy0", "yy1", "lpv0", "lpv1")
+    for a, b in ((0, s), (s, 3), (3, 4)):
+        if b > a:
+            iota(T.kx[:, 4 * a:4 * b], [[1, b - a], [100, 2], [-100, 2]], order[a], "kx%d" % a)
+    kxs = tuple(k for k in ("kx0", "kx%d" % s, "kx3") if k in lastw)
+    iota(T.k16[:], [[0, 8], [1, 16], [0, 2]], 0, "k16")
+    iota(T.kst[:], [[0, 8], [1, 16], [16, 2]], 1, "kst")
+    iota(T.kc[:], [[128, 4], [-1, 2], [64, 2]], 32, "kc")
+    h10 = ("h100", "h101")
+    iota(T.hot10[:], [[0, 20]], 1, *h10)
+    select(T.hot10[:], T.hot10[:], [[32, 2], [-16, 10]], Op.is_ge, 0.0, 0, 1, h10, h10)
+    select(T.hot10[:], T.hot10[:], [[-32, 2], [16, 10]], Op.is_ge, 0.0, 15, -1, h10, h10)
+    select(T.hot10[:, 10:20], T.hot10[:, 10:20], [[0, 10]], Op.is_ge, 0.0, -96, 1, h10, h10)
+    iota(T.colw[:], [[16, 12]], 0, "colw")
+
+    kk = ("kq", "kp", "kqo", "kpo")
+    for j in (0, 4, 3, 2, 1):
+        mm(j, 128, "x", 32 + 32 * j, "k", 64, rd=kk)
+    best = [T.rmax[:, 127:128], T.rmax[:, 255:256]]
+    top = {j: (T.m5[:, j:j + 1], "m%d" % j) for j in (2, 3, 4)}
+    top[0], top[1] = (best[0], "r0"), (best[1], "r1")
+
+    def lift(j):
+        m, k = top[j]
+        act(T.a5[:, j:j + 1], m, Act.Abs, (k,), ("a5%d" % j,), scale=EPS, bias=TINY)
+
+    def spread(j, c, mask, mk):
+        m, k = top[j]
+        act(T.rep[:, c:c + 32], mask, Act.Identity, (mk, k, "a5%d" % j), ("rep%d" % c,), scale=T.a5[:, j:j + 1], bias=m)
+
+    def below(i, dst, a, step):
+        end = 128 - (step > 1)
+        n = len(range(a, end, step))
+        act(T.jnk[:, 128 * i:128 * i + n], T.rmax[:, 128 * i + a:128 * i + end:step], Act.Sign, ("r%d" % i,),
+            (dst + str(i), "jnk%d" % i), scale=-1.0, bias=best[i], accum_out=tn(dst, i))
+
+    def scan(i):
+        vscan(T.rmax[:, 128 * i:128 * i + 128], bank(i, 128), T.zt[:, D1:D1 + 128], -1e29, Op.max, Op.add,
+              ("b%d" % i, "zt"), ("r%d" % i,))
+
+    def count(i):
+        c = slice(160 * i, 160 * i + 160)
+        act(T.cj[:, c], T.cc[:, c], Act.Copy, ("cc%d" % i,), ("cj%d" % i, "cn%d" % i), scale=1.0 / 64, accum_out=tn("cn", i))
+
+    scan(0)
+    lift(0)
+    spread(0, 0, T.tri32[:], "tri32")
+    below(0, "gg", 0, 1)
+    for j in (4, 3, 2):
+        vred(top[j][0], bank(j, 128), Op.max, ("b%d" % j,), (top[j][1],))
+    act(T.a5[:, 2:5], T.m5[:, 2:5], Act.Abs, ("m2", "m3", "m4"), ("a52", "a53", "a54"), scale=EPS, bias=TINY)
+    for j in (4, 3):
+        spread(j, 32 * j, T.mk[:, 32 * j - 64:32 * j - 32], "mk")
+    scan(1)
+    lift(1)
+    spread(1, 192, T.tri32[:], "tri32")
+    for b in range(4):
+        mm(b, 128, "e", 128 * b, "a", 0, True, False, lrd=("eq%d" % b, "ep%d" % b))
+    below(1, "gg", 0, 1)
+    below(0, "gq", 31, 32)
+    below(1, "gq", 31, 32)
+    vts(T.rep[:, 160:192], T.mk[:, 0:32], T.a5[:, 0:1], best[0], Op.mult, Op.add, ("mk", "r0", "a50"), ("rep160",))
+    vts(T.rep[:, 64:96], T.mk[:, 0:32], T.a5[:, 2:3], top[2][0], Op.mult, Op.add, ("mk", "m2", "a52"), ("rep64",))
+    vts(T.rep[:, 32:64], T.rowb[:, 0:32], 0.0, best[1], Op.mult, Op.add, ("rowb", "r1"), ("rep32",))
+    vtr(T.mrow[:, 0:160], T.rep[:, 0:160], tuple("rep%d" % c for c in range(0, 160, 32)), ("mrow0",))
+    vtr(T.mrow[:, 160:224], T.rep[:, 160:224], ("rep160", "rep192"), ("mrow1",))
+    vts(T.cc[:, 0:160], T.mrow[:, 0:160], best[0], None, Op.is_gt, rd=("mrow0", "r0"), wr=("cc0",))
+    vts(T.cc[:, 160:320], T.mrow[:, 64:224], best[1], None, Op.is_gt, rd=("mrow0", "mrow1", "r1"), wr=("cc1",))
+    count(0)
+    count(1)
+
+    def mzb(k, c):
+        vts(T.zt[:, 16 * k - 15:16 * k + 16:2], T.kx[:], tn("gq", 1), cs(c), Op.is_equal, Op.mult,
+            kxs + ("gq1", "c%d" % c), ("mm%d" % k,))
+
+    vcp(T.trt[96:128, 513:640:4], T.trt[96:128, 384:512:4], ("trA", "trB"), ("trB",))
+    quant("tr", 0, 160, T.trt[:], ("trA", "trB", "trB2"))
+    for i in range(2):
+        vts(T.ot[:, i:512:4], T.rowb[:], tn("gg", i), tn("cn", i), Op.is_equal, Op.is_gt,
+            ("rowb", "gg%d" % i, "cn%d" % i), ("ot" + "AB"[i],))
+        vts(T.ot[:, 512 + i:528:4], T.rowb[:, 0:4], tn("gq", i), tn("cn", i), Op.is_equal, Op.is_gt,
+            ("rowb", "gq%d" % i, "cn%d" % i), ("ot" + "CD"[i],))
+        if i == 0:
+            mzb(1, 1)
+    quant("ob", 0, 134, T.ot[:], ("otA", "otB", "otC", "otD", "otZ"))
+    mm(5, 134, "tr", 0, "ob", 0)
+    mm(6, 134, "tr", 32, "ob", 0)
+    act(T.kab[:], T.kx[:], Act.Abs, kxs + ("gq0",), ("kab",), scale=-1.0, bias=tn("gq", 0))
+    act(T.zt[:, 0:32:2], T.kab[:], Act.Relu, ("kab", "c1", "c8"), ("mm0",), scale=cs(8), bias=cs(1))
+    act(T.zt[:, 32:64:2], T.kab[:], Act.Relu, ("kab", "c6", "c9"), ("mm2",), scale=cs(9), bias=cs(6))
+    mzb(3, 7)
+    quant("mm", 0, 136, T.zt[:, 0:544], ("mm0", "mm1", "mm2", "mm3", "zt"))
+    below(0, "gd", 15, 16)
+    below(1, "gd", 15, 16)
+    for i in range(2):
+        act(tn("gm", i), tn("gd", i), Act.Identity, ("gd%d" % i, "gg%d" % i), ("gm%d" % i,), scale=-16.0, bias=tn("gg", i))
+    act(tn("gd64"), tn("gd"), Act.Copy, ("gd0", "gd1"), ("gd64",), scale=64.0)
+    c = _TINY["yy"]
+    vred(T.tiny[:, c:c + 1], bank(5, 128, 133), Op.max, ("b5",), ("yy0",))
+    vred(T.tiny[96:128, c + 1:c + 2], T.psum[96:128, 6 * 512 + 128:6 * 512 + 133], Op.max, ("b6",), ("yy1",))
+    for i in range(2):
+        vts(T.stt[:, i:512:2], T.kst[:], tn("yy", i), None, Op.is_equal, rd=("kst", "yy%d" % i), wr=("st%d" % i,))
+
+    def s2(i):
+        vts(T.s2t[:, i:512:2], T.k16[:], tn("gm", i), None, Op.is_equal, rd=("k16", "gm%d" % i), wr=("s2%d" % i,))
+
+    s2(0)
+    quant("st", 0, 128, T.stt[:], ("st0", "st1"))
+    s2(1)
+    mm(7, 128, "st", 0, "mm", 0, True, False)
+    mm(7, 128, "st", 0, "mm", 8, False, True)
+    y2 = ("yy0", "yy1")
+    act(tn("thy"), tn("yy"), Act.Sign, y2, ("thy",))
+    c = _TINY["lpv"]
+    act(T.jnk[:, 0:128], bank(5, 128), Act.Relu, ("b5", "yy0"), ("lpv0", "jnk0"), accum_out=T.tiny[:, c:c + 1])
+    act(T.jnk[96:128, 128:256], T.psum[96:128, 6 * 512:6 * 512 + 128], Act.Relu, ("b6", "yy1"), ("lpv1", "jnk1"),
+        accum_out=T.tiny[96:128, c + 1:c + 2])
+    act(tn("sg1"), tn("yy"), Act.Sign, y2, ("sg1",), bias=-16.5)
+    act(tn("yl8"), tn("yy"), Act.Copy, y2, ("yl8",), bias=-8.0)
+    for i in range(2):
+        act(tn("key", i), tn("lpv", i), Act.Identity, ("lpv%d" % i, "thy", "gd64"), ("key%d" % i,),
+            scale=tn("thy", i), bias=tn("gd64", i))
+    act(tn("hi"), tn("sg1"), Act.Copy, ("sg1",), ("hi",), scale=8.0, bias=32.0 * (3 - s) + 8.0)
+    for i in range(2):
+        act(tn("lo", i), tn("sg1", i), Act.Identity, ("sg1", "yl8"), ("lo%d" % i,), scale=-8.0, bias=tn("yl8", i))
+    quant("s2", 0, 128, T.s2t[:], ("s20", "s21"))
+    for i in range(2):
+        vts(T.zt[:, D2 + 2 + i:D2 + 64:4], T.kc[:], tn("key", i), tn("hi", i), Op.is_equal, Op.mult,
+            ("kc", "key%d" % i, "hi"), ("m2%d" % (2 + i),))
+    for i in range(2):
+        vts(T.zt[:, D2 + i:D2 + 64:4], T.kc[:], tn("key", i), tn("lo", i), Op.is_equal, Op.mult,
+            ("kc", "key%d" % i, "lo%d" % i), ("m2%d" % i,))
+    vcp(T.invu[:], bank(7, 8), ("b7",), ("invu",))
+    quant("m2", 0, 128, T.zt[:, D2 + 64 - 512:D2 + 64], ("zt", "m20", "m21", "m22", "m23"))
+    mm(4, 128, "s2", 0, "m2", 0)
+    pickq("sl", 0, 96, "x", 0, 192, T.invu[:, 0:6], ("xq", "invu"), ("slq",))
+    pickp("sl", 0, 96, "x", 0, 192, T.invu[:, 0:6], ("xp", "invu"), ("slp",))
+    at = 128 + 32 * (3 - s)
+    vcp(T.lst[:], bank(4, 112, 128), ("b4",), ("lst",))
+    scatter([T.lst[:, 4 * r:4 * r + 4] for r in others], T.ll[:, 8 * s:8 * s + 4], others, "li", "lb", ("lst",), 3)
+    scatter([T.slq[:, 32 * i:32 * i + 32].bitcast(u8) for i in range(3)], T.winq[:, at:at + 32].bitcast(u8), others,
+            "so", "lb", ("slq",), 0)
+    scatter([T.slp[:, 32 * i:32 * i + 32] for i in range(3)], T.winp[:, at:at + 32], others, "so", "lb", ("slp",), 2)
+    lastw["winq"] = lastw["winp"] = [("so", 24)]
+    lastw["lli"] = [("li", 12)]
+    if s < 3:
+        act(T.nz[:], T.lst[:], Act.Sign, ("lst",), ("nz",))
+    pickp("win", at, at + 32, "x", 0, 192, T.invu[:, 6:8], ("xp", "invu"), ("winpo",))
+    act(tn("thz"), tn("lpv"), Act.Relu, ("lpv0", "lpv1"), ("thz",), scale=2.0, bias=-60.0)
+    act(tn("gd16"), tn("gd"), Act.Copy, ("gd0", "gd1"), ("gd16",), scale=16.0)
+    for i in range(2):
+        act(tn("thr", i), tn("thz", i), Act.Copy, ("thz", "thy"), ("thr%d" % i,), scale=tn("thy", i))
+    for i in range(2):
+        hj = T.hot10[:, 10 * i:10 * i + 10]
+        act(T.tmt[:, 640 + i:680:4], hj, Act.Copy, ("h10%d" % i, "gm%d" % i), ("tm%d" % (2 + i),), scale=tn("gm", i))
+        act(T.tmt[:, 642 + i:680:4], hj, Act.Copy, ("h10%d" % i, "gd16"), ("tm%d" % (4 + i),), scale=tn("gd16", i))
+    act(T.tmt[:, 0:512:4], T.et[:, 3:515:4], Act.Copy, ("et", "thr0"), ("tm0",), scale=tn("thr", 0))
+    act(T.tmt[:, 513:640:4], T.et[:, 387:515:4], Act.Copy, ("et", "thr1"), ("tm1",), scale=tn("thr", 1))
+    act(T.colw[:], T.colw[:], Act.Identity, ("colw", "c1"), ("colw",), bias=cs(1))
+    HB = (5, 6, 7, 4)
+
+    def hot(i):
+        act(T.hot[:, i:768:4], bank(HB[i], 192), Act.Relu, ("b%d" % HB[i],), ("hot%d" % i,), scale=0.0625)
+
+    for i in (0, 3, 1, 2):
+        quant("w", 128 * i, 128 * i + 128, T.wt[:, 512 * i:512 * i + 512], ("wt",), ("wq%d" % i, "wp%d" % i))
+        mm(HB[i], 192, "w", 128 * i, "x", 0, lrd=("wq%d" % i, "wp%d" % i))
+        if i == 3 and s < 3:
+            for h in range(2):
+                vtt(T.csum[:, h:8:2], T.nz[:, h:16:4], T.nz[:, 2 + h:16:4], Op.add, ("nz",), ("csum%d" % h,))
+            higher = [r for r in others if r > s]
+            scatter([T.csum[:, 0:8]] * len(higher), T.lc[:, 8 * s:8 * s + 8], higher, "ct", "lb", ("csum0", "csum1"), 1)
+    vcp(T.ll[:, 8 * s:8 * s + 4], T.lst[:, 4 * s:4 * s + 4], ("lst", "ll"), ("llo",))
+    pickq("win", at, at + 32, "x", 0, 192, T.invu[:, 6:8], ("xq", "invu"), ("winqo",))
+    hot(0)
+    hot(3)
+    act(T.colm[:], T.colw[:], Act.Copy, ("colw",), ("colm",), bias=-192.0)
+    iota(T.rst[:], [[0, 160]], 1, "rst")
+    select(T.rst[:], T.rst[:], [[0, 10], [1, 16]], Op.not_equal, 0.0, 0, 0, ("rst",), ("rst",))
+    iota(T.mgt[:, 0:192], [[0, 192]], -1, "mgta")
+    iota(T.mgt[:, 192:320], [[192, 4], [1, 32]], 0, "mgtb")
+    iota(T.mgr[:, 0:32], [[0, 32]], -1, "mgr0")
+
+    L, X = T.ll, T.lab
+    rl = ("ll", "llo", "lli")
+    vtt(X[:, 0:32:2], L[:, 0:16], L[:, 16:32], Op.max, rl, ("lab0",))
+    vtt(X[:, 1:32:2], L[:, 0:16], L[:, 16:32], Op.min, rl, ("lab1",))
+    vtt(T.lu[:], X[:, 0:16], X[:, 16:32], Op.max, ("lab0", "lab1"), ("lu",))
+    vtt(T.lcm[:], X[:, 0:4:2], X[:, 16:20:2], Op.min, ("lab0",), ("lcm",))
+    vtt(T.lf[:], T.lu[:, 1:4:2], T.lu[:, 4:8:2], Op.max, ("lu",), ("lf",))
+    vts(T.off[:, 0:2], T.lu[:, 0:4:2], 127.0, None, Op.add, rd=("lu",), wr=("off0",))
+    for h in range(2):
+        vts(T.off[:, 2 + h:3 + h], T.lcm[:, h:h + 1], T.lf[:, h:h + 1], 127.0, Op.max, Op.add, ("lcm", "lf"), ("off%d" % (1 + h),))
+
+    def ww(c):
+        return ("win" + c, "win" + c + "o", "win" + c + "z", "off0", "off1", "off2")
+    pickq("k", 0, 64, "win", 0, 256, T.off[:, 0:4], ww("q"), ("kqf",))
+    pickp("k", 0, 64, "win", 0, 256, T.off[:, 0:4], ww("p"), ("kpf",))
+    for b in range(4):
+        mm(b, 128, "e", 128 * b, "k", 0, False, True, rd=kk + ("kqf", "kpf"), lrd=("eq%d" % b, "ep%d" % b))
+    hot(1)
+    if s > 0:
+        lastw["lc"] = [("ct", 4 * s)]
+    for i in range(2):
+        vts(T.s3t[:, i:512:2], T.k16[:], cs(1), None, Op.is_equal, rd=("k16", "c1"), wr=("s3%d" % i,))
+    quant("tm", 0, 172, T.tmt[:], tuple("tm%d" % i for i in range(6)))
+    quant("s3", 0, 128, T.s3t[:], ("s30", "s31"))
+    vcp(T.colu[:], T.colw[:], ("colw",), ("colu",))
+    mm(5, 128, "s3", 0, "tm", 44)
+    mm(4, 160, "s3", 0, "tm", 0)
+    for b in range(4):
+        act(T.ss[:, 32 * b:32 * b + 32], bank(b, 32, 64), Act.Copy, ("b%d" % b,), ("ss%d" % b,))
+    for b in range(4):
+        vtt(T.mh[:, b:128:4], T.ss[:, 32 * b:32 * b + 32], bank(b, 32), Op.add, ("ss%d" % b, "b%d" % b), ("mt%d" % b,))
+    quant("m", 0, 128, T.mh[:, 0:512], ("mt0", "mt1", "mt2", "mt3", "mhz"))
+    for i in range(4):
+        mm(i, 128, "w", 128 * i, "m", 0, lrd=("wq%d" % i, "wp%d" % i))
+    vcp(T.gwu[:], bank(5, 116, 126), ("b5",), ("gwu",))
+    if s > 0:
+        src, key = T.lc[:, 0:8], "lc"
+        for r in range(1, s):
+            vtt(T.ctot[:], src, T.lc[:, 8 * r:8 * r + 8], Op.add, ("lc", key), ("ctot",))
+            src, key = T.ctot[:], "ctot"
+        vcp(T.cu[:], src, (key,), ("cu",))
+        act(T.crow[:], T.rowb[:, 0:128].indirect(T.cu[:, 0:8]), Act.Copy, ("rowb", "cu"), ("crow",))
+    vtt(T.dw[:], bank(5, 116, 126), T.colm[:, 2:12], Op.subtract, ("b5", "colm"), ("dw",))
+    vts(T.hot[:, 2:768:4], bank(HB[2], 192), 0.0, 0.0625, Op.max, Op.mult, ("b%d" % HB[2],), ("hot2",))
+    for i in range(4):
+        k = ("b%d" % i,), ("hmt%d" % i,)
+        if i % 2 == 0:
+            act(T.mh[:, 512 + i:640:4], bank(i, 32), Act.Relu, k[0], k[1], scale=0.0625)
+        else:
+            vts(T.mh[:, 512 + i:640:4], bank(i, 32), 0.0, 0.0625, Op.max, Op.mult, k[0], k[1])
+    if s > 0:
+        act(T.prior[:], T.crow[:, 0:128].indirect(T.gwu[:, 0:10]), Act.Copy, ("crow", "gwu"), ("prior",))
+    quant("hm", 0, 128, T.mh[:, 128:640], ("mhz", "hmt0", "hmt1", "hmt2", "hmt3"))
+    hat = 192 + A * s
+    bcast(T.hmq[:, 96:128].bitcast(u8), T.hwq[:, hat:hat + A].bitcast(u8), "hm", "lb", ("hmq",))
+    bcast(T.hmp[:, 96:128], T.hwp[:, hat:hat + A], "hm", "lb", ("hmp",))
+    lastw["hwq"] = lastw["hwp"] = [("hm", 96)]
+    pickp("hw", hat, hat + A, "hm", 96, 128, T.colu[:, 0:2], ("hmp", "colu"), ("hwpm",))
+
+    quant("hw", 0, 192, T.hot[:], ("hot0", "hot1", "hot2", "hot3"), ("hwqo", "hwpo"))
+    if s > 0:
+        vtt(T.adm[:], T.prior[:], bank(4, 160), Op.is_lt, ("prior", "b4"), ("adm",))
+    else:
+        vts(T.adm[:], bank(4, 160), 0.0, None, Op.is_gt, rd=("b4",), wr=("adm",))
+    vts(T.fm[:], T.lu[:, 0:4:2], 0.0, 192.0 + A * s, Op.is_gt, Op.mult, ("lu",), ("fm",))
+    vscan(T.scn[:], T.rst[:], T.adm[:], 0.0, Op.mult, Op.add, ("rst", "adm"), ("scn",))
+    vtt(T.fin[:, 0:2], T.fm[:], T.colw[:, 0:2], Op.add, ("fm", "colw"), ("fin0",))
+    vtt(T.admt[:], T.scn[:, 15:160:16], T.dw[:], Op.mult, ("scn", "dw"), ("admt",))
+    vtt(T.fin[:, 2:12], T.admt[:], T.colw[:, 2:12], Op.add, ("admt", "colw"), ("fin1",))
+    pickq("hw", hat, hat + A, "hm", 96, 128, T.colu[:, 0:2], ("hmq", "colu"), ("hwqm",))
+    vcp(T.finu[:], T.fin[:], ("fin0", "fin1"), ("finu",))
+    quant("v", 0, 128, T.vt[:], ("vt",))
+
+    def hh(c):
+        return ("hw" + c, "hw" + c + "m", "hw" + c + "o", "finu")
+    for i, (a, b) in enumerate([(0, 128), (128, 192)]):
+        pickq("fo", a, b, "hw", 0, 320, T.finu[:, a // 16:b // 16], hh("q"), ("foq%d" % i,))
+        pickp("fo", a, b, "hw", 0, 320, T.finu[:, a // 16:b // 16], hh("p"), ("fop%d" % i,))
+    sync(T.oc[:, 0:768], T.foq[:, 0:192].bitcast(u8), "dout", ("foq0", "foq1"))
+    for k in range(4):
+        sync(T.osc[4 * k:4 * k + 4, 0:192], T.fop[32 * k:32 * k + 4, 0:192], "dout", ("fop0", "fop1"))
+    mm(6, 128, "v", 0, "fo", 0, rd=("foq0", "fop0"))
+    mm(7, 128, "v", 0, "fo", 64, rd=("foq0", "fop0", "foq1", "fop1"))
+    act(T.mgr[:, 32:192], T.mgt[:, 0:320].indirect(T.finu[:, 2:12]), Act.Copy, ("mgta", "mgtb", "finu"), ("mgr1",))
+    run("s", lambda: S.dma_start(T.mg[0:1, 0:192], T.mgr[0:1, 0:192]), ("mgr0", "mgr1"), (), sem="dout")
+    vcp(T.yo[:, 0:128], bank(6, 128), ("b6",), ("yo0",))
+    sync(T.y[:, 0:128], T.yo[:, 0:128], "dout", ("yo0",))
+    vcp(T.yo[:, 128:192], bank(7, 64, 128), ("b7",), ("yo1",))
+    sync(T.y[:, 128:192], T.yo[:, 128:192], "dout", ("yo1",))
+    wait("g", [(n, total[n]) for n in ("qv", "qs", "qt", "qg", "dout")] + [("lb", lsum["lb"])])

@@ -20,21 +20,32 @@ def _mx(**names):
 
 
 SCRATCH["psum"] = ("psum", [128, 4096], F)
-_sb(F, cst=16, th=8, kc=16, kx=16, colw=12, colm=12, mk=96, tri32=32, rst=160, mgt=320,
-    rmax=256, m5=8, a5=8, rep=224, mrow=224, jnk=256, tiny=64, kab=16,
-    ss=128, dw=10, crow=128, prior=160, adm=160, scn=160, admt=10, fin=12, fm=2, mgr=192, yo=192)
-_sb("int32", pidi=1, ui=1)
-_sb(B16, rowb=128, k16=256, kst=256, et=516, trt=640, s3t=512, zt=664, xz=512, xt=1152, wt=2048, vt=512,
-    cc=320, cj=320, ot=536, stt=512, s2t=512, tmt=688, mh=640, hot=768, hot10=20,
-    lst=16, nz=16, csum=8, ll=32, lc=24, lab=32, lu=16, lcm=2, lf=2, ctot=8)
+_sb(F, cst=16, kc=16, kcx=32, kx=16, col0=12, colw=12, colm=12, mk=4, th=4, tri32=32, rst=160, mgt=320,
+    r0=224, rx=640, a5=2, mrow=224, jnk=256, tiny=64, kab=16, ps=288,
+    ss=64, dw=10, crow=128, prior=160, adm=160, scn=160, admt=10, fin=12, fm=2, mgr=192, ya=320, yo=192)
+_sb("int32", ui=4)
+_sb(B16, rowb=128, r10=10, rsm=138, k16=128, kst=256, et=516, trt=640, s3t=512, zt=664, xt=1152, wt=2048, vt=512,
+    cc=320, cj=160, ot=552, stt=512, s2t=512, tmt=688, mh=640, hot=768, hot10=20,
+    lst=16, nz=16, csum=8, ll=32, lc=24, lab=32, lu=16, lcm=2, ctot=8)
 _sb(U16, colu=12, invu=8, off=4, gwu=10, cu=8, finu=12)
-_mx(e=512, tr=160, s3=128, a=128, x=288, k=192, w=512, v=128, ob=134, mm=136, st=128, s2=128, m2=128, tm=172,
-    sl=96, win=256, m=128, hm=128, hw=320, fo=192)
+_mx(e=512, tr=160, s3=128, x=416, k=224, w=512, v=128, ob=138, mm=136, st=128, s2=128, m2=128, tm=172,
+    sl=96, win=160, m=128, hm=128, hw=320, fo=192)
 
-SEMAPHORES = ["qv", "qs", "qt", "qg", "dxa", "dx", "dx2", "dw", "dv", "dz1", "dz2", "dz3", "dz4", "dkq", "dkp", "dzq", "dzp",
+SEMAPHORES = ["qv", "qs", "qt", "qg", "dxa", "dx", "dw", "dv", "dz1", "dz2", "dz3", "dz4", "dz5", "dz6", "dz7", "dzq", "dzp",
               "an", "so", "li", "ct", "hm", "la", "lb", "dout"]
-_TINY = {n: 2 * i for i, n in enumerate(["cn", "gg", "gd", "gq", "gm", "gd16", "gd64", "yy", "lpv", "key", "hi", "yl8", "lo",
-                                         "thz", "thy", "thr", "sg1"])}
+_TINY = {n: 2 * i for i, n in enumerate(["cn", "gg", "gd", "gq", "gm", "gd16", "gd64", "thz", "thy", "thr"])}
+ORDER = """
+zt ui0 mk ll ui3 ui1 xzz psz ui2 et kxa kc col0 xza aq c0 rowb k16 c6 xt otC colu et.2 tri32 kpo c8 s31 s30 colw otA
+kqo eq2 s32 eq0 xq s33 trA trB to_aq to_ap h10 kpd c7 kxb tr1 kqd b1 c9 kxc otE mk.2 xq2 eq3 eq1 r1 colm tri32.2 b0 rsm
+r0 b3 b4 gg1 a50 trB2 r3 tm1 winpz tm0 wt r4 a51 b2 r2 w3 r10 dg0 dg1 trA.2 h10.2 trA.3 h10.3 rsm.2 th trB.2 mgr0 w4
+gg0 w2 w1 gq1 gq0 h10.4 w0 ca4 ca2 ca3 ca0 gd1 cn0 cb0 cb1 kab gm1 mgta rst trq rst.2 kst mm1 cn1 mm3 gd0 mm2 gm0 mm0
+otA.2 otC.2 otB gd64 otD s23 s21 b0.2 b1.2 obq b2.2 b5 s20 s22 mmq s2q ps0 b6 ps1 kc0 m20 m22 kc1 m23 m21 mhz winqz st0
+vt gd16 tm3 thz mgtb b3.2 st1 m2q stq b4.2 b7 thy tm4 wq2 thr1 thr0 b7.2 lst wq3 invu slq tm1.2 nz csum1 b4.3 to_lst
+wq1 s3q llo b7.3 csum0 wq0 winqo b6.2 b5.2 lab0 to_slq winpo slp lab1 tm5 tm2 hot2 tm0.2 hot3 hot0 lcm lu off1 to_slp
+off0 off2 to_csum0 fm vq kqf kpf b0.3 fin0 b1.3 hot1 b2.3 b2.4 b3.3 ss0 tmq lc ctot ctot.2 b3.4 b4.4 b5.3 mt2 mt0 ss1
+mt1 mt3 cu mq gwu crow b2.5 b0.4 b3.5 hmt2 b1.4 dw hwqo hmt3 hmt1 b6.3 hmt0 prior hmq to_hmq ya0 adm hwqm to_hmp hwpm
+scn admt fin1 finu mgr1 mg foq b7.4 ya1 oc fop osc.3 osc.2 osc osc.4 yo1 yo0 y
+""".split()
 
 
 def rank_program(g, core, T, topo):
@@ -44,34 +55,12 @@ def rank_program(g, core, T, topo):
     others = [r for r in range(4) if r != s]
     order = others + [s]
     Q = {"v": g.vector, "s": g.scalar, "t": g.tensor, "g": g, "y": g.sync}
-    waited, lastw, readers, total = {q: {} for q in Q}, {}, {}, {}
+    ops, seen = [], {}
 
-    def wait(q, toks):
-        need = {}
-        for n, val in toks:
-            need[n] = max(need.get(n, 0), val)
-        for n in sorted(need):
-            if waited[q].get(n, 0) < need[n]:
-                Q[q].wait_ge(T.sem[n], need[n])
-                waited[q][n] = need[n]
-
-    def run(q, fn, rd=(), wr=(), sem=None, free=()):
-        toks = []
-        for k in rd:
-            toks += lastw[k]
-        for k in wr:
-            if k not in free:
-                toks += lastw.get(k, []) + readers.get(k, [])
-        wait(q, toks)
-        n, inc = (sem, 16) if sem else ("q" + q, 1)
-        fn().then_inc(T.sem[n], inc)
-        total[n] = total.get(n, 0) + inc
-        tok = (n, total[n])
-        for k in rd:
-            readers.setdefault(k, []).append(tok)
-        for k in wr:
-            lastw[k] = [tok]
-            readers[k] = []
+    def run(q, fn, rd=(), wr=(), sem=None, free=(), name=None, arr=None):
+        n = name or wr[0]
+        seen[n] = seen.get(n, 0) + 1
+        ops.append((n if seen[n] == 1 else "%s.%d" % (n, seen[n]), q, fn, tuple(rd), tuple(wr), sem, free, arr))
 
     V, S, P = g.vector, g.scalar, g.tensor
 
@@ -102,14 +91,14 @@ def rank_program(g, core, T, topo):
     def act(out, in_, func, rd=(), wr=(), **kw):
         run("s", lambda: S.activation(out, in_, func, **kw), rd, wr)
 
-    def iota(out, pattern, base, *wr, rd=(), cm=0):
-        run("g", lambda: g.iota(out, pattern, base, cm, allow_small_or_imprecise_dtypes=True), rd, wr)
+    def iota(out, pattern, base, *wr, cm=0):
+        run("g", lambda: g.iota(out, pattern, base, cm, allow_small_or_imprecise_dtypes=True), (), wr)
 
-    def select(out, in_, pattern, op, fl, base, cm, rd, wr):
-        run("g", lambda: g.affine_select(out, in_, pattern, op, fl, base, cm), rd, wr)
+    def select(out, pattern, op, fl, base, cm, *wr):
+        run("g", lambda: g.affine_select(out, out, pattern, op, fl, base, cm), wr, wr)
 
-    def sync(out, in_, sem, rd=(), wr=()):
-        run("y", lambda: g.sync.dma_start(out, in_), rd, wr, sem=sem)
+    def sync(out, in_, sem, rd=(), wr=(), name=None):
+        run("y", lambda: g.sync.dma_start(out, in_), rd, wr, sem=sem, name=name)
 
     def quant(n, a, b, src, rd=(), wr=None):
         run("v", lambda: V.quantize_mx(T[n + "q"][:, a:b], T[n + "p"][:, a:b], src), rd, wr or (n + "q", n + "p"))
@@ -143,24 +132,21 @@ def rank_program(g, core, T, topo):
 
     lsum = {"la": 0, "lb": 0}
 
-    def bcast(src, dst, sem, local, rd):
+    def bcast(src, dst, sem, local, rd, arr):
         eng = topo.engines(core, T.cores[others[0]])
-        wait("g", [t for k in rd for t in lastw[k]])
-        g.remote_dma_fused([RemoteDMATransfer(dst_ids=[addr(r) for r in others], dma_engine_mask=msk(eng),
-                                              remote_sem=T.sem[sem], srcs=[src], dsts=[dst] * len(others))],
-                           local_sem=T.sem[local])
+        tr = [RemoteDMATransfer(dst_ids=[addr(r) for r in others], dma_engine_mask=msk(eng), remote_sem=T.sem[sem],
+                                srcs=[src], dsts=[dst] * len(others))]
         lsum[local] += len(eng)
+        run("g", lambda: g.remote_dma_fused(tr, local_sem=T.sem[local]), rd, tuple(arr), name="to_" + rd[0], arr=arr)
 
-    def scatter(srcs, dst, dests, sem, local, rd, first=0):
-        wait("g", [t for k in rd for t in lastw[k]])
+    def scatter(srcs, dst, dests, sem, local, rd, masks, arr):
         tr = []
-        for i, (r, src) in enumerate(zip(dests, srcs)):
+        for r, src in zip(dests, srcs):
             eng = topo.engines(core, T.cores[r])
-            j = 4 * ((first + i) % 4)
-            tr.append(RemoteDMATransfer(dst_ids=[addr(r)], dma_engine_mask=msk(eng[j:j + 4]), remote_sem=T.sem[sem],
-                                        src=src, dst=dst))
-        g.remote_dma_fused(tr, local_sem=T.sem[local])
-        lsum[local] += 4 * len(tr)
+            es = [e for j in masks[(r - s) % 4] for e in eng[4 * j:4 * j + 4]]
+            tr.append(RemoteDMATransfer(dst_ids=[addr(r)], dma_engine_mask=msk(es), remote_sem=T.sem[sem], src=src, dst=dst))
+            lsum[local] += len(es)
+        run("g", lambda: g.remote_dma_fused(tr, local_sem=T.sem[local]), rd, tuple(arr), name="to_" + rd[0], arr=arr)
 
     u8 = dt.uint8
 
@@ -168,246 +154,229 @@ def rank_program(g, core, T, topo):
         return T.cst[:, j:j + 1]
 
     D1, D2 = 64, 600
-    Z = T.zt[:, D1:D2]
 
-    sync(T.xz[:, 0:128], T.x[:, 0:128], "dxa", (), ("xza",))
-    run("s", lambda: S.dma_start(T.xt[:, 0:768], T.x[:, :]), (), ("xt",), sem="dx")
-    sync(T.xt[:, 768:1152], T.x[:, 128:512], "dx2", (), ("xt2",))
+    def zeros(n):
+        return T.zt[:, D1:D1 + n]
 
-    run("g", lambda: g.iota(T.pidi[:], [[0, 1]], 0, 1), (), ("pidi",))
-    iota(cs(0), [[0, 1]], 0, "c0", cm=1)
+    X0 = 96
+    sync(T.xt[:, 384:512], T.x[:, 0:128], "dxa", (), ("xza",))
+    sync(T.xt[:, 512:1152], T.x[:, 128:768], "dx", (), ("xt",))
+    run("g", lambda: g.iota(T.ui[:, 0:1], [[0, 1]], 0, 1), (), ("ui0",))
     iota(T.rowb[:], [[1, 128]], 0, "rowb")
+    iota(T.col0[:], [[16, 12]], 0, "col0")
 
-    fill(T.xz[:, 128:512], 0.0, "xzz")
-    run("v", lambda: V.tensor_scalar(T.ui[:], T.pidi[:], 31, None, Op.bitwise_and), ("pidi",), ("ui",))
-    fill(Z, 0.0, "zt")
-    vcp(cs(2), T.ui[:], ("ui",), ("c2",))
+    def bits(j, op, c):
+        run("v", lambda: V.tensor_scalar(T.ui[:, j:j + 1], T.ui[:, 0:1], c, None, op), ("ui0",), ("ui%d" % j,))
+
+    fill(T.xt[:, 0:384], 0.0, "xzz")
+    bits(1, Op.bitwise_and, 15)
+    bits(2, Op.bitwise_and, 31)
+    bits(3, Op.logical_shift_right, 4)
+    fill(zeros(536), 0.0, "zt")
+    vcp(T.cst[:, 0:4], T.ui[:], ("ui0", "ui1", "ui2", "ui3"), ("c0", "c1", "c2", "c3"))
     fill(T.ll[:], 0.0, "ll")
-    quant("a", 0, 128, T.xz[:], ("xza", "xzz"))
-    at1 = 64 + A * s
-    bcast(T.aq[:, 0:A].bitcast(u8), T.kq[:, at1:at1 + A].bitcast(u8), "an", "la", ("aq",))
-    bcast(T.ap[:, 0:A], T.kp[:, at1:at1 + A], "an", "la", ("ap",))
-    lastw["kq"] = lastw["kp"] = [("an", 96)]
-    iota(T.th[:, 0:7], [[0, 7]], 1, "th")
-    select(T.th[:, 0:7], T.th[:, 0:7], [[-16, 7]], Op.is_ge, 0.0, -16, 1, ("th",), ("th",))
-    sync(T.kq[:, at1:at1 + A].bitcast(u8), T.aq[:, 0:A].bitcast(u8), "dkq", ("aq",), ("kqo",))
-    sync(T.kp[:, at1:at1 + A], T.ap[:, 0:A], "dkp", ("ap",), ("kpo",))
-    wait("y", [("la", lsum["la"])])
-    sync(T.ot[:, 0:536], Z, "dz4", ("zt",), ("otA", "otB", "otC", "otD", "otZ"))
-    sync(T.wt[:, :], T.w[:, :], "dw", (), ("wt",))
-    sync(T.winq[:, 96:128].bitcast(u8), T.aq[:, 96:128].bitcast(u8), "dzq", ("aq",), ("winqz",))
-    sync(T.winp[:, 96:128], T.ap[:, 96:128], "dzp", ("ap",), ("winpz",))
-    sync(T.tmt[:, 0:512], T.zt[:, D1:D1 + 512], "dz2", ("zt",), ("tm0",))
-    sync(T.tmt[:, 512:688], T.zt[:, D1:D1 + 176], "dz3", ("zt",), ("tm1",))
-    sync(T.mh[:, 128:512], T.zt[:, D1:D1 + 384], "dz1", ("zt",), ("mhz",))
-    sync(T.vt[:, :], T.v[:, :], "dv", (), ("vt",))
-    for i in range(2, 6):
-        lastw["tm%d" % i] = list(lastw["tm1"])
+    quant("x", 0, 128, T.xt[:, 0:512], ("xza", "xzz", "ll"), ("aq", "ap"))
+    at1 = A * s
+    bcast(T.xq[:, X0:X0 + A].bitcast(u8), T.kq[:, at1:at1 + A].bitcast(u8), "an", "la", ("aq",), {"kq": ("an", 96)})
+    bcast(T.xp[:, X0:X0 + A], T.kp[:, at1:at1 + A], "an", "la", ("ap",), {"kp": ("an", 96), "la": ("la", 32)})
+    vts(T.colu[:], T.col0[:], cs(1), None, Op.add, rd=("col0", "c1"), wr=("colu",))
+    vts(T.colw[:], T.col0[:], cs(1), None, Op.add, rd=("col0", "c1"), wr=("colw",))
+    for c, k in ((at1, "o"), (128, "d")):
+        pickq("k", c, c + A, "x", X0, X0 + A, T.colu[:, 0:2], ("aq", "colu"), ("kq" + k,))
+        pickp("k", c, c + A, "x", X0, X0 + A, T.colu[:, 0:2], ("ap", "colu"), ("kp" + k,))
+    sync(T.trt[:, 0:512], zeros(512), "dz5", ("zt",), ("trA",))
+    sync(T.trt[:, 512:640], zeros(128), "dz6", ("zt",), ("trB", "trB2", "tr1"))
+    sync(T.ot[:, 0:40], zeros(40), "dz7", ("zt",), ("otC", "otD", "otE"))
+    sync(T.ot[:, 40:552], zeros(512), "dz4", ("zt",), ("otA", "otB"))
+    sync(T.wt[:, :], T.w[:, :], "dw", ("la",), ("wt",))
+    sync(T.winq[:, 0:32].bitcast(u8), T.xq[:, 0:32].bitcast(u8), "dzq", ("aq", "la"), ("winqz",))
+    sync(T.winp[:, 0:32], T.xp[:, 0:32], "dzp", ("ap", "la"), ("winpz",))
+    sync(T.tmt[:, 0:512], zeros(512), "dz2", ("zt", "la"), ("tm0",))
+    sync(T.tmt[:, 512:688], zeros(176), "dz3", ("zt", "la"), ("tm1", "tm2", "tm3", "tm4", "tm5"))
+    sync(T.mh[:, 128:512], zeros(384), "dz1", ("zt", "la"), ("mhz",))
+    sync(T.vt[:, :], T.v[:, :], "dv", ("la",), ("vt",))
 
     fill(T.et[:], 0.0, "et")
     vts(T.et[:, 3:515:4], T.rowb[:], cs(0), 0.5, Op.is_equal, Op.mult, ("rowb", "c0"), ("et",))
-    quant("x", 0, 288, T.xt[:], ("xt", "xt2"))
+    quant("x", 128, 288, T.xt[:, 512:1152], ("xt",))
+    quant("x", 288, 416, T.xt[:, 512:1024], ("xt",), ("xq2", "xp2"))
     for b in range(4):
         quant("e", 128 * b, 128 * b + 128, T.et[:, 3 - b:515 - b], ("et",), ("eq%d" % b, "ep%d" % b))
-    act(T.mk[:], T.zt[:, D1:D1 + 96], Act.Copy, ("zt",), ("mk",), bias=1.0)
-    act(T.trt[:, 0:512], T.zt[:, D1:D1 + 512], Act.Copy, ("zt",), ("trA",))
-    act(T.trt[:, 512:640], T.zt[:, D1:D1 + 128], Act.Copy, ("zt",), ("trB", "trB2"))
     act(T.tri32[:], T.rowb[:, 0:32], Act.Sign, ("rowb", "c2"), ("tri32",), scale=-1.0, bias=cs(2))
     act(T.tri32[:], T.tri32[:], Act.Relu, ("tri32",), ("tri32",), scale=-1.0)
-    act(T.jnk[:, 128:135], T.th[:, 0:7], Act.Copy, ("th",), ("jnk1", "c3"), accum_out=cs(3))
-    act(cs(1), cs(3), Act.Identity, ("c3", "c0"), ("c1",), scale=-16.0, bias=cs(0))
     act(cs(6), cs(3), Act.Copy, ("c3",), ("c6",), scale=16.0, bias=32.0)
     act(cs(7), cs(3), Act.Copy, ("c3",), ("c7",), scale=16.0, bias=64.0)
     act(cs(8), cs(1), Act.Copy, ("c1",), ("c8",), scale=-1.0)
     act(cs(9), cs(3), Act.Copy, ("c3",), ("c9",), scale=-16.0, bias=-32.0)
-    select(T.mk[:], T.mk[:], [[32, 3], [0, 32]], Op.is_ge, 0.0, -96, 1, ("mk",), ("mk",))
+    act(T.ps[0:96, 144:282], T.zt[0:96, D1:D1 + 138], Act.Copy, ("zt",), ("psz",))
+    act(T.rsm[:], zeros(138), Act.Copy, ("zt",), ("rsm",), bias=1.0)
+    act(T.trt[:, 2:640:4], zeros(160), Act.Copy, ("zt", "trA"), ("tr1",), bias=1.0)
+    iota(T.mk[:, 0:3], [[0, 3]], -1, "mk")
+    select(T.mk[:, 0:3], [[32, 3]], Op.is_ge, 0.0, -96, 1, "mk")
     tp = [[-1, 128]]
-    select(T.trt[:, 0:512:4], T.trt[:, 0:512:4], tp, Op.is_ge, -1.0, 0, 1, ("trA",), ("trA",))
-    select(T.trt[:, 0:512:4], T.trt[:, 0:512:4], tp, Op.not_equal, 32.0, 0, 1, ("trA",), ("trA",))
+    select(T.trt[:, 0:512:4], tp, Op.is_ge, -1.0, 0, 1, "trA")
+    select(T.trt[:, 0:512:4], tp, Op.not_equal, 32.0, 0, 1, "trA")
     iota(T.trt[:, 512:640:4], [[0, 32]], -1, "trB2")
-    c = _TINY["yy"]
-    iota(T.tiny[:, c:c + 4], [[0, 4]], 0, "yy0", "yy1", "lpv0", "lpv1")
+    iota(T.r10[:], [[0, 2], [1, 5]], 0, "r10")
+    select(T.rsm[:, 0:10], [[0, 2], [1, 5]], Op.not_equal, 0.0, -4, 0, "rsm")
+    select(T.ot[:, 2:16:4], [[0, 4]], Op.is_ge, -1.0, -17, 1, "otE")
     for a, b in ((0, s), (s, 3), (3, 4)):
         if b > a:
-            iota(T.kx[:, 4 * a:4 * b], [[1, b - a], [100, 2], [-100, 2]], order[a], "kx%d" % a)
-    kxs = tuple(k for k in ("kx0", "kx%d" % s, "kx3") if k in lastw)
-    iota(T.k16[:], [[0, 8], [1, 16], [0, 2]], 0, "k16")
+            iota(T.kx[:, 4 * a:4 * b], [[1, b - a], [100, 2], [-100, 2]], order[a], "kx" + "abc"[(a > 0) + (a == 3)])
+    kxs = ("kxa", "kxb", "kxc") if 0 < s < 3 else ("kxa", "kxc")
+    iota(T.k16[:], [[0, 8], [1, 16]], 0, "k16")
     iota(T.kst[:], [[0, 8], [1, 16], [16, 2]], 1, "kst")
     iota(T.kc[:], [[128, 4], [-1, 2], [64, 2]], 32, "kc")
-    h10 = ("h100", "h101")
-    iota(T.hot10[:], [[0, 20]], 1, *h10)
-    select(T.hot10[:], T.hot10[:], [[32, 2], [-16, 10]], Op.is_ge, 0.0, 0, 1, h10, h10)
-    select(T.hot10[:], T.hot10[:], [[-32, 2], [16, 10]], Op.is_ge, 0.0, 15, -1, h10, h10)
-    select(T.hot10[:, 10:20], T.hot10[:, 10:20], [[0, 10]], Op.is_ge, 0.0, -96, 1, h10, h10)
-    iota(T.colw[:], [[16, 12]], 0, "colw")
+    iota(T.hot10[:], [[0, 20]], 1, "h10")
+    select(T.hot10[:], [[32, 2], [-16, 10]], Op.is_ge, 0.0, 0, 1, "h10")
+    select(T.hot10[:], [[-32, 2], [16, 10]], Op.is_ge, 0.0, 15, -1, "h10")
+    select(T.hot10[:, 10:20], [[0, 10]], Op.is_ge, 0.0, -96, 1, "h10")
+    for t in range(4):
+        vts(T.s3t[:, t:512:4], T.k16[:], cs(1), None, Op.is_equal, rd=("k16", "c1"), wr=("s3%d" % t,))
+    quant("s3", 0, 128, T.s3t[:], ("s30", "s31", "s32", "s33"))
+    vcp(T.trt[96:128, 513:640:4], T.trt[96:128, 384:512:4], ("trA",), ("trB",))
+    quant("tr", 0, 160, T.trt[:], ("trA", "trB", "trB2", "tr1"))
 
-    kk = ("kq", "kp", "kqo", "kpo")
-    for j in (0, 4, 3, 2, 1):
-        mm(j, 128, "x", 32 + 32 * j, "k", 64, rd=kk)
-    best = [T.rmax[:, 127:128], T.rmax[:, 255:256]]
-    top = {j: (T.m5[:, j:j + 1], "m%d" % j) for j in (2, 3, 4)}
-    top[0], top[1] = (best[0], "r0"), (best[1], "r1")
-
-    def lift(j):
-        m, k = top[j]
-        act(T.a5[:, j:j + 1], m, Act.Abs, (k,), ("a5%d" % j,), scale=EPS, bias=TINY)
-
-    def spread(j, c, mask, mk):
-        m, k = top[j]
-        act(T.rep[:, c:c + 32], mask, Act.Identity, (mk, k, "a5%d" % j), ("rep%d" % c,), scale=T.a5[:, j:j + 1], bias=m)
+    kk = ("kq", "kp", "kqo", "kpo", "kqd", "kpd")
+    run_max = [T.r0] + [T.rx] * 4
+    o = [0, 0, 160, 320, 480]
+    best = [T.r0[:, 159:160], T.rx[:, 159:160]]
+    for j in (0, 1, 4, 3, 2):
+        mm(j, 160, "x", 128 + 32 * j, "k", 0, rd=kk, lrd=("xq", "xp", "xq2", "xp2") if j > 1 else None)
+    for j in (0, 1, 4, 3, 2):
+        vscan(run_max[j][:, o[j]:o[j] + 160], bank(j, 160), zeros(160), -1e29, Op.max, Op.add, ("b%d" % j, "zt"), ("r%d" % j,))
 
     def below(i, dst, a, step):
         end = 128 - (step > 1)
         n = len(range(a, end, step))
-        act(T.jnk[:, 128 * i:128 * i + n], T.rmax[:, 128 * i + a:128 * i + end:step], Act.Sign, ("r%d" % i,),
+        act(T.jnk[:, 128 * i:128 * i + n], run_max[i][:, a:end:step], Act.Sign, ("r%d" % i,),
             (dst + str(i), "jnk%d" % i), scale=-1.0, bias=best[i], accum_out=tn(dst, i))
 
-    def scan(i):
-        vscan(T.rmax[:, 128 * i:128 * i + 128], bank(i, 128), T.zt[:, D1:D1 + 128], -1e29, Op.max, Op.add,
-              ("b%d" % i, "zt"), ("r%d" % i,))
-
-    def count(i):
-        c = slice(160 * i, 160 * i + 160)
-        act(T.cj[:, c], T.cc[:, c], Act.Copy, ("cc%d" % i,), ("cj%d" % i, "cn%d" % i), scale=1.0 / 64, accum_out=tn("cn", i))
-
-    scan(0)
-    lift(0)
-    spread(0, 0, T.tri32[:], "tri32")
-    below(0, "gg", 0, 1)
-    for j in (4, 3, 2):
-        vred(top[j][0], bank(j, 128), Op.max, ("b%d" % j,), (top[j][1],))
-    act(T.a5[:, 2:5], T.m5[:, 2:5], Act.Abs, ("m2", "m3", "m4"), ("a52", "a53", "a54"), scale=EPS, bias=TINY)
-    for j in (4, 3):
-        spread(j, 32 * j, T.mk[:, 32 * j - 64:32 * j - 32], "mk")
-    scan(1)
-    lift(1)
-    spread(1, 192, T.tri32[:], "tri32")
+    for i in range(2):
+        a5 = T.a5[:, i:i + 1]
+        act(a5, best[i], Act.Abs, ("r%d" % i,), ("a5%d" % i,), scale=EPS, bias=TINY)
+        act(T.r0[:, 192 - 32 * i:224 - 32 * i], T.tri32[:], Act.Identity, ("tri32", "r%d" % i, "a5%d" % i), ("dg%d" % i,),
+            scale=a5, bias=best[i])
+    act(T.th[:, 0:3], T.mk[:, 0:3], Act.Identity, ("mk", "r0", "a50"), ("th",), scale=T.a5[:, 0:1], bias=best[0])
+    for i in range(2):
+        below(i, "gg", 0, 1)
+        below(i, "gq", 31, 32)
+        below(i, "gd", 15, 16)
     for b in range(4):
-        mm(b, 128, "e", 128 * b, "a", 0, True, False, lrd=("eq%d" % b, "ep%d" % b))
-    below(1, "gg", 0, 1)
-    below(0, "gq", 31, 32)
-    below(1, "gq", 31, 32)
-    vts(T.rep[:, 160:192], T.mk[:, 0:32], T.a5[:, 0:1], best[0], Op.mult, Op.add, ("mk", "r0", "a50"), ("rep160",))
-    vts(T.rep[:, 64:96], T.mk[:, 0:32], T.a5[:, 2:3], top[2][0], Op.mult, Op.add, ("mk", "m2", "a52"), ("rep64",))
-    vts(T.rep[:, 32:64], T.rowb[:, 0:32], 0.0, best[1], Op.mult, Op.add, ("rowb", "r1"), ("rep32",))
-    vtr(T.mrow[:, 0:160], T.rep[:, 0:160], tuple("rep%d" % c for c in range(0, 160, 32)), ("mrow0",))
-    vtr(T.mrow[:, 160:224], T.rep[:, 160:224], ("rep160", "rep192"), ("mrow1",))
-    vts(T.cc[:, 0:160], T.mrow[:, 0:160], best[0], None, Op.is_gt, rd=("mrow0", "r0"), wr=("cc0",))
-    vts(T.cc[:, 160:320], T.mrow[:, 64:224], best[1], None, Op.is_gt, rd=("mrow0", "mrow1", "r1"), wr=("cc1",))
-    count(0)
-    count(1)
+        mm(b, 128, "e", 128 * b, "x", 0, True, False, rd=("aq", "ap"), lrd=("eq%d" % b, "ep%d" % b))
+    vtr(T.mrow[:, 192:224], T.rx[:, 128:160], ("r1",), ("w1",))
+    for j in (4, 3):
+        vtr(T.mrow[:, 32 * j - 64:32 * j - 32], T.rx[:, o[j] + 128:o[j] + 160], ("r%d" % j,), ("w%d" % j,))
+    vtr(T.mrow[:, 96:192], T.r0[:, 128:224], ("r0", "dg0", "dg1"), ("w0",))
+    vtr(T.mrow[:, 0:32], T.rx[:, o[2] + 128:o[2] + 160], ("r2",), ("w2",))
+    U = 1.0 / 64
+    vts(T.cc[:, 96:160], T.mrow[:, 160:224], best[0], U, Op.is_gt, Op.mult, ("w0", "w1", "r0"), ("ca0",))
+    for j in (4, 3, 2):
+        c = slice(32 * j - 64, 32 * j - 32)
+        vts(T.cc[:, c], T.mrow[:, c], T.th[:, j - 2:j - 1], U, Op.is_gt, Op.mult, ("w%d" % j, "th"), ("ca%d" % j,))
+    vts(T.cc[:, 288:320], T.mrow[:, 128:160], best[1], U, Op.is_gt, Op.mult, ("w0", "r1"), ("cb0",))
+    vts(T.cc[:, 160:288], T.mrow[:, 0:128], best[1], U, Op.is_ge, Op.mult, ("w0", "w2", "w3", "w4", "r1"), ("cb1",))
+    act(T.cj[:], T.cc[:, 0:160], Act.Copy, ("ca0", "ca2", "ca3", "ca4"), ("cn0",), accum_out=tn("cn", 0))
+    vred(tn("cn", 1), T.cc[:, 160:320], Op.add, ("cb0", "cb1"), ("cn1",))
 
     def mzb(k, c):
         vts(T.zt[:, 16 * k - 15:16 * k + 16:2], T.kx[:], tn("gq", 1), cs(c), Op.is_equal, Op.mult,
             kxs + ("gq1", "c%d" % c), ("mm%d" % k,))
 
-    vcp(T.trt[96:128, 513:640:4], T.trt[96:128, 384:512:4], ("trA", "trB"), ("trB",))
-    quant("tr", 0, 160, T.trt[:], ("trA", "trB", "trB2"))
-    for i in range(2):
-        vts(T.ot[:, i:512:4], T.rowb[:], tn("gg", i), tn("cn", i), Op.is_equal, Op.is_gt,
-            ("rowb", "gg%d" % i, "cn%d" % i), ("ot" + "AB"[i],))
-        vts(T.ot[:, 512 + i:528:4], T.rowb[:, 0:4], tn("gq", i), tn("cn", i), Op.is_equal, Op.is_gt,
-            ("rowb", "gq%d" % i, "cn%d" % i), ("ot" + "CD"[i],))
-        if i == 0:
-            mzb(1, 1)
-    quant("ob", 0, 134, T.ot[:], ("otA", "otB", "otC", "otD", "otZ"))
-    mm(5, 134, "tr", 0, "ob", 0)
-    mm(6, 134, "tr", 32, "ob", 0)
     act(T.kab[:], T.kx[:], Act.Abs, kxs + ("gq0",), ("kab",), scale=-1.0, bias=tn("gq", 0))
     act(T.zt[:, 0:32:2], T.kab[:], Act.Relu, ("kab", "c1", "c8"), ("mm0",), scale=cs(8), bias=cs(1))
     act(T.zt[:, 32:64:2], T.kab[:], Act.Relu, ("kab", "c6", "c9"), ("mm2",), scale=cs(9), bias=cs(6))
+    mzb(1, 1)
     mzb(3, 7)
     quant("mm", 0, 136, T.zt[:, 0:544], ("mm0", "mm1", "mm2", "mm3", "zt"))
-    below(0, "gd", 15, 16)
-    below(1, "gd", 15, 16)
+    act(tn("gd64"), tn("gd"), Act.Copy, ("gd0", "gd1"), ("gd64",), scale=-64.0)
     for i in range(2):
         act(tn("gm", i), tn("gd", i), Act.Identity, ("gd%d" % i, "gg%d" % i), ("gm%d" % i,), scale=-16.0, bias=tn("gg", i))
-    act(tn("gd64"), tn("gd"), Act.Copy, ("gd0", "gd1"), ("gd64",), scale=64.0)
-    c = _TINY["yy"]
-    vred(T.tiny[:, c:c + 1], bank(5, 128, 133), Op.max, ("b5",), ("yy0",))
-    vred(T.tiny[96:128, c + 1:c + 2], T.psum[96:128, 6 * 512 + 128:6 * 512 + 133], Op.max, ("b6",), ("yy1",))
+        act(T.kcx[:, 16 * i:16 * i + 16], T.kc[:], Act.Identity, ("kc", "gd64"), ("kc%d" % i,), bias=tn("gd64", i))
+    at = 32 * (4 - s)
     for i in range(2):
-        vts(T.stt[:, i:512:2], T.kst[:], tn("yy", i), None, Op.is_equal, rd=("kst", "yy%d" % i), wr=("st%d" % i,))
+        vts(T.s2t[:, i:512:4], T.k16[:], tn("gm", i), None, Op.is_equal, rd=("k16", "gm%d" % i), wr=("s2%d" % i,))
+        vts(T.s2t[:, 2 + i:512:4], T.k16[:], tn("gm", i), at + 16.0, Op.is_equal, Op.mult, ("k16", "gm%d" % i), ("s2%d" % (2 + i),))
+    quant("s2", 0, 128, T.s2t[:], ("s20", "s21", "s22", "s23"))
 
-    def s2(i):
-        vts(T.s2t[:, i:512:2], T.k16[:], tn("gm", i), None, Op.is_equal, rd=("k16", "gm%d" % i), wr=("s2%d" % i,))
+    for i in range(2):
+        vts(T.ot[:, 40 + i:552:4], T.rowb[:], tn("gg", i), tn("cn", i), Op.is_equal, Op.is_gt,
+            ("rowb", "gg%d" % i, "cn%d" % i), ("ot" + "AB"[i],))
+        vts(T.ot[:, i:40:4], T.r10[:], tn("gq", i), tn("cn", i), Op.is_equal, Op.is_gt,
+            ("r10", "gq%d" % i, "cn%d" % i), ("ot" + "CD"[i],))
+    quant("ob", 0, 138, T.ot[:], ("otA", "otB", "otC", "otD", "otE"))
+    mm(5, 138, "tr", 0, "ob", 0)
+    mm(6, 138, "tr", 32, "ob", 0)
+    vscan(T.ps[:, 0:138], bank(5, 138), T.rsm[:], -17.0, Op.max, Op.mult, ("b5", "rsm"), ("ps0",))
+    vscan(T.ps[96:128, 144:282], T.psum[96:128, 6 * 512:6 * 512 + 138], T.rsm[96:128, :], -17.0, Op.max, Op.mult,
+          ("b6", "rsm"), ("ps1",))
+    pk = (("ps0",), ("ps1", "psz"))
 
-    s2(0)
-    quant("st", 0, 128, T.stt[:], ("st0", "st1"))
-    s2(1)
-    mm(7, 128, "st", 0, "mm", 0, True, False)
-    mm(7, 128, "st", 0, "mm", 8, False, True)
-    y2 = ("yy0", "yy1")
-    act(tn("thy"), tn("yy"), Act.Sign, y2, ("thy",))
-    c = _TINY["lpv"]
-    act(T.jnk[:, 0:128], bank(5, 128), Act.Relu, ("b5", "yy0"), ("lpv0", "jnk0"), accum_out=T.tiny[:, c:c + 1])
-    act(T.jnk[96:128, 128:256], T.psum[96:128, 6 * 512:6 * 512 + 128], Act.Relu, ("b6", "yy1"), ("lpv1", "jnk1"),
-        accum_out=T.tiny[96:128, c + 1:c + 2])
-    act(tn("sg1"), tn("yy"), Act.Sign, y2, ("sg1",), bias=-16.5)
-    act(tn("yl8"), tn("yy"), Act.Copy, y2, ("yl8",), bias=-8.0)
+    def pc(i, c):
+        return T.ps[:, 144 * i + c:144 * i + c + 1]
+
     for i in range(2):
-        act(tn("key", i), tn("lpv", i), Act.Identity, ("lpv%d" % i, "thy", "gd64"), ("key%d" % i,),
-            scale=tn("thy", i), bias=tn("gd64", i))
-    act(tn("hi"), tn("sg1"), Act.Copy, ("sg1",), ("hi",), scale=8.0, bias=32.0 * (3 - s) + 8.0)
-    for i in range(2):
-        act(tn("lo", i), tn("sg1", i), Act.Identity, ("sg1", "yl8"), ("lo%d" % i,), scale=-8.0, bias=tn("yl8", i))
-    quant("s2", 0, 128, T.s2t[:], ("s20", "s21"))
-    for i in range(2):
-        vts(T.zt[:, D2 + 2 + i:D2 + 64:4], T.kc[:], tn("key", i), tn("hi", i), Op.is_equal, Op.mult,
-            ("kc", "key%d" % i, "hi"), ("m2%d" % (2 + i),))
-    for i in range(2):
-        vts(T.zt[:, D2 + i:D2 + 64:4], T.kc[:], tn("key", i), tn("lo", i), Op.is_equal, Op.mult,
-            ("kc", "key%d" % i, "lo%d" % i), ("m2%d" % i,))
-    vcp(T.invu[:], bank(7, 8), ("b7",), ("invu",))
+        kc = T.kcx[:, 16 * i:16 * i + 16]
+        vts(T.zt[:, D2 + 2 + i:D2 + 64:4], kc, pc(i, 137), pc(i, 8), Op.is_equal, Op.min, pk[i] + ("kc%d" % i,), ("m2%d" % (2 + i),))
+        vts(T.zt[:, D2 + i:D2 + 64:4], kc, pc(i, 137), pc(i, 3), Op.is_equal, Op.mult, pk[i] + ("kc%d" % i,), ("m2%d" % i,))
     quant("m2", 0, 128, T.zt[:, D2 + 64 - 512:D2 + 64], ("zt", "m20", "m21", "m22", "m23"))
     mm(4, 128, "s2", 0, "m2", 0)
-    pickq("sl", 0, 96, "x", 0, 192, T.invu[:, 0:6], ("xq", "invu"), ("slq",))
-    pickp("sl", 0, 96, "x", 0, 192, T.invu[:, 0:6], ("xp", "invu"), ("slp",))
-    at = 128 + 32 * (3 - s)
-    vcp(T.lst[:], bank(4, 112, 128), ("b4",), ("lst",))
-    scatter([T.lst[:, 4 * r:4 * r + 4] for r in others], T.ll[:, 8 * s:8 * s + 4], others, "li", "lb", ("lst",), 3)
+    for i in range(2):
+        vts(T.stt[:, i:512:2], T.kst[:], pc(i, 8), None, Op.is_equal, rd=pk[i] + ("kst",), wr=("st%d" % i,))
+    quant("st", 0, 128, T.stt[:], ("st0", "st1"))
+    vts(T.lst[:], bank(4, 112, 128), 0.0, None, Op.max, rd=("b4",), wr=("lst",))
+    mm(7, 128, "st", 0, "mm", 0, True, False)
+    mm(7, 128, "st", 0, "mm", 8, False, True)
+    vcp(T.invu[:], bank(7, 8), ("b7",), ("invu",))
+    pickq("sl", 0, 96, "x", X0, X0 + 192, T.invu[:, 0:6], ("xq", "aq", "invu"), ("slq",))
+    pickp("sl", 0, 96, "x", X0, X0 + 192, T.invu[:, 0:6], ("xp", "ap", "invu"), ("slp",))
+    scatter([T.lst[:, 4 * r:4 * r + 4] for r in others], T.ll[:, 8 * s:8 * s + 4], others, "li", "lb", ("lst",),
+            {1: (0, 1), 2: (2,), 3: (3,)}, {"lli": ("li", 16)})
     scatter([T.slq[:, 32 * i:32 * i + 32].bitcast(u8) for i in range(3)], T.winq[:, at:at + 32].bitcast(u8), others,
-            "so", "lb", ("slq",), 0)
-    scatter([T.slp[:, 32 * i:32 * i + 32] for i in range(3)], T.winp[:, at:at + 32], others, "so", "lb", ("slp",), 2)
-    lastw["winq"] = lastw["winp"] = [("so", 24)]
-    lastw["lli"] = [("li", 12)]
+            "so", "lb", ("slq",), {1: (2, 3), 2: (0,), 3: (1,)}, {"winq": ("so", 32)})
+    scatter([T.slp[:, 32 * i:32 * i + 32] for i in range(3)], T.winp[:, at:at + 32], others, "so", "lb", ("slp",),
+            {1: (0, 1), 2: (2,), 3: (3,)}, {"winp": ("so", 32)})
+    p2 = ("ps0", "ps1", "psz")
     if s < 3:
         act(T.nz[:], T.lst[:], Act.Sign, ("lst",), ("nz",))
-    pickp("win", at, at + 32, "x", 0, 192, T.invu[:, 6:8], ("xp", "invu"), ("winpo",))
-    act(tn("thz"), tn("lpv"), Act.Relu, ("lpv0", "lpv1"), ("thz",), scale=2.0, bias=-60.0)
+    pickp("win", at, at + 32, "x", X0, X0 + 192, T.invu[:, 6:8], ("xp", "ap", "invu"), ("winpo",))
+    act(tn("thy"), T.ps[:, 8:153:144], Act.Sign, p2, ("thy",))
+    act(tn("thz"), T.ps[:, 137:282:144], Act.Relu, p2, ("thz",), scale=2.0, bias=-60.0)
     act(tn("gd16"), tn("gd"), Act.Copy, ("gd0", "gd1"), ("gd16",), scale=16.0)
     for i in range(2):
         act(tn("thr", i), tn("thz", i), Act.Copy, ("thz", "thy"), ("thr%d" % i,), scale=tn("thy", i))
     for i in range(2):
         hj = T.hot10[:, 10 * i:10 * i + 10]
-        act(T.tmt[:, 640 + i:680:4], hj, Act.Copy, ("h10%d" % i, "gm%d" % i), ("tm%d" % (2 + i),), scale=tn("gm", i))
-        act(T.tmt[:, 642 + i:680:4], hj, Act.Copy, ("h10%d" % i, "gd16"), ("tm%d" % (4 + i),), scale=tn("gd16", i))
+        act(T.tmt[:, 640 + i:680:4], hj, Act.Copy, ("h10", "gm%d" % i), ("tm%d" % (2 + i),), scale=tn("gm", i))
+        act(T.tmt[:, 642 + i:680:4], hj, Act.Copy, ("h10", "gd16"), ("tm%d" % (4 + i),), scale=tn("gd16", i))
     act(T.tmt[:, 0:512:4], T.et[:, 3:515:4], Act.Copy, ("et", "thr0"), ("tm0",), scale=tn("thr", 0))
     act(T.tmt[:, 513:640:4], T.et[:, 387:515:4], Act.Copy, ("et", "thr1"), ("tm1",), scale=tn("thr", 1))
-    act(T.colw[:], T.colw[:], Act.Identity, ("colw", "c1"), ("colw",), bias=cs(1))
+    if s < 3:
+        for h in range(2):
+            vtt(T.csum[:, h:8:2], T.nz[:, h:16:4], T.nz[:, 2 + h:16:4], Op.add, ("nz",), ("csum%d" % h,))
+        higher = [r for r in others if r > s]
+        scatter([T.csum[:, 0:8]] * len(higher), T.lc[:, 8 * s:8 * s + 8], higher, "ct", "lb", ("csum0", "csum1"),
+                {1: (1,), 2: (2,), 3: (3,)}, {})
     HB = (5, 6, 7, 4)
-
-    def hot(i):
-        act(T.hot[:, i:768:4], bank(HB[i], 192), Act.Relu, ("b%d" % HB[i],), ("hot%d" % i,), scale=0.0625)
-
-    for i in (0, 3, 1, 2):
+    for i in range(4):
         quant("w", 128 * i, 128 * i + 128, T.wt[:, 512 * i:512 * i + 512], ("wt",), ("wq%d" % i, "wp%d" % i))
-        mm(HB[i], 192, "w", 128 * i, "x", 0, lrd=("wq%d" % i, "wp%d" % i))
-        if i == 3 and s < 3:
-            for h in range(2):
-                vtt(T.csum[:, h:8:2], T.nz[:, h:16:4], T.nz[:, 2 + h:16:4], Op.add, ("nz",), ("csum%d" % h,))
-            higher = [r for r in others if r > s]
-            scatter([T.csum[:, 0:8]] * len(higher), T.lc[:, 8 * s:8 * s + 8], higher, "ct", "lb", ("csum0", "csum1"), 1)
+        mm(HB[i], 192, "w", 128 * i, "x", X0, rd=("xq", "xp", "aq", "ap"), lrd=("wq%d" % i, "wp%d" % i))
+        act(T.hot[:, i:768:4], bank(HB[i], 192), Act.Relu, ("b%d" % HB[i],), ("hot%d" % i,), scale=0.0625)
     vcp(T.ll[:, 8 * s:8 * s + 4], T.lst[:, 4 * s:4 * s + 4], ("lst", "ll"), ("llo",))
-    pickq("win", at, at + 32, "x", 0, 192, T.invu[:, 6:8], ("xq", "invu"), ("winqo",))
-    hot(0)
-    hot(3)
+    pickq("win", at, at + 32, "x", X0, X0 + 192, T.invu[:, 6:8], ("xq", "aq", "invu"), ("winqo",))
     act(T.colm[:], T.colw[:], Act.Copy, ("colw",), ("colm",), bias=-192.0)
     iota(T.rst[:], [[0, 160]], 1, "rst")
-    select(T.rst[:], T.rst[:], [[0, 10], [1, 16]], Op.not_equal, 0.0, 0, 0, ("rst",), ("rst",))
+    select(T.rst[:], [[0, 10], [1, 16]], Op.not_equal, 0.0, 0, 0, "rst")
     iota(T.mgt[:, 0:192], [[0, 192]], -1, "mgta")
     iota(T.mgt[:, 192:320], [[192, 4], [1, 32]], 0, "mgtb")
     iota(T.mgr[:, 0:32], [[0, 32]], -1, "mgr0")
+    quant("tm", 0, 172, T.tmt[:], tuple("tm%d" % i for i in range(6)))
+    mm(5, 128, "s3", 0, "tm", 44)
+    mm(4, 160, "s3", 0, "tm", 0)
+    quant("hw", 0, 192, T.hot[:], ("hot0", "hot1", "hot2", "hot3"), ("hwqo", "hwpo"))
+    quant("v", 0, 128, T.vt[:], ("vt",))
+    mm(6, 192, "v", 0, "hw", 0, rd=("hwqo", "hwpo"))
+    act(T.ya[:, 0:192], bank(6, 192), Act.Copy, ("b6",), ("ya0",))
 
     L, X = T.ll, T.lab
     rl = ("ll", "llo", "lli")
@@ -415,61 +384,53 @@ def rank_program(g, core, T, topo):
     vtt(X[:, 1:32:2], L[:, 0:16], L[:, 16:32], Op.min, rl, ("lab1",))
     vtt(T.lu[:], X[:, 0:16], X[:, 16:32], Op.max, ("lab0", "lab1"), ("lu",))
     vtt(T.lcm[:], X[:, 0:4:2], X[:, 16:20:2], Op.min, ("lab0",), ("lcm",))
-    vtt(T.lf[:], T.lu[:, 1:4:2], T.lu[:, 4:8:2], Op.max, ("lu",), ("lf",))
-    vts(T.off[:, 0:2], T.lu[:, 0:4:2], 127.0, None, Op.add, rd=("lu",), wr=("off0",))
+    vcp(T.off[:, 2:4], T.lu[:, 0:4:2], ("lu",), ("off0",))
     for h in range(2):
-        vts(T.off[:, 2 + h:3 + h], T.lcm[:, h:h + 1], T.lf[:, h:h + 1], 127.0, Op.max, Op.add, ("lcm", "lf"), ("off%d" % (1 + h),))
+        vts(T.off[:, h:h + 1], T.lcm[:, h:h + 1], T.lu[:, 1 + 2 * h:2 + 2 * h], T.lu[:, 4 + 2 * h:5 + 2 * h], Op.max, Op.max,
+            ("lcm", "lu"), ("off%d" % (1 + h),))
 
     def ww(c):
-        return ("win" + c, "win" + c + "o", "win" + c + "z", "off0", "off1", "off2")
-    pickq("k", 0, 64, "win", 0, 256, T.off[:, 0:4], ww("q"), ("kqf",))
-    pickp("k", 0, 64, "win", 0, 256, T.off[:, 0:4], ww("p"), ("kpf",))
+        return ("winq", "winp", "win" + c + "o", "win" + c + "z", "off0", "off1", "off2")
+    pickq("k", 160, 224, "win", 0, 160, T.off[:, 0:4], ww("q"), ("kqf",))
+    pickp("k", 160, 224, "win", 0, 160, T.off[:, 0:4], ww("p"), ("kpf",))
     for b in range(4):
-        mm(b, 128, "e", 128 * b, "k", 0, False, True, rd=kk + ("kqf", "kpf"), lrd=("eq%d" % b, "ep%d" % b))
-    hot(1)
-    if s > 0:
-        lastw["lc"] = [("ct", 4 * s)]
-    for i in range(2):
-        vts(T.s3t[:, i:512:2], T.k16[:], cs(1), None, Op.is_equal, rd=("k16", "c1"), wr=("s3%d" % i,))
-    quant("tm", 0, 172, T.tmt[:], tuple("tm%d" % i for i in range(6)))
-    quant("s3", 0, 128, T.s3t[:], ("s30", "s31"))
-    vcp(T.colu[:], T.colw[:], ("colw",), ("colu",))
-    mm(5, 128, "s3", 0, "tm", 44)
-    mm(4, 160, "s3", 0, "tm", 0)
-    for b in range(4):
-        act(T.ss[:, 32 * b:32 * b + 32], bank(b, 32, 64), Act.Copy, ("b%d" % b,), ("ss%d" % b,))
-    for b in range(4):
-        vtt(T.mh[:, b:128:4], T.ss[:, 32 * b:32 * b + 32], bank(b, 32), Op.add, ("ss%d" % b, "b%d" % b), ("mt%d" % b,))
+        ee = ("eq%d" % b, "ep%d" % b)
+        mm(b, 128, "e", 128 * b, "k", 96, False, b < 2, rd=kk + ("kqf", "kpf"), lrd=ee)
+        if b >= 2:
+            mm(b, 128, "e", 128 * b, "k", 64, False, True, rd=kk + ("kqf", "kpf"), lrd=ee)
+    for b in range(2):
+        act(T.ss[:, 32 * b:32 * b + 32], bank(b, 64, 96), Act.Copy, ("b%d" % b,), ("ss%d" % b,))
+    vcp(T.mh[:, 2:128:4], bank(2, 96, 128), ("b2",), ("mt2",))
+    for b in range(2):
+        vtt(T.mh[:, b:128:4], T.ss[:, 32 * b:32 * b + 32], bank(b, 96, 128), Op.add, ("ss%d" % b, "b%d" % b), ("mt%d" % b,))
+    vcp(T.mh[:, 3:128:4], bank(3, 96, 128), ("b3",), ("mt3",))
     quant("m", 0, 128, T.mh[:, 0:512], ("mt0", "mt1", "mt2", "mt3", "mhz"))
     for i in range(4):
         mm(i, 128, "w", 128 * i, "m", 0, lrd=("wq%d" % i, "wp%d" % i))
-    vcp(T.gwu[:], bank(5, 116, 126), ("b5",), ("gwu",))
-    if s > 0:
-        src, key = T.lc[:, 0:8], "lc"
-        for r in range(1, s):
-            vtt(T.ctot[:], src, T.lc[:, 8 * r:8 * r + 8], Op.add, ("lc", key), ("ctot",))
-            src, key = T.ctot[:], "ctot"
-        vcp(T.cu[:], src, (key,), ("cu",))
-        act(T.crow[:], T.rowb[:, 0:128].indirect(T.cu[:, 0:8]), Act.Copy, ("rowb", "cu"), ("crow",))
-    vtt(T.dw[:], bank(5, 116, 126), T.colm[:, 2:12], Op.subtract, ("b5", "colm"), ("dw",))
-    vts(T.hot[:, 2:768:4], bank(HB[2], 192), 0.0, 0.0625, Op.max, Op.mult, ("b%d" % HB[2],), ("hot2",))
     for i in range(4):
         k = ("b%d" % i,), ("hmt%d" % i,)
         if i % 2 == 0:
             act(T.mh[:, 512 + i:640:4], bank(i, 32), Act.Relu, k[0], k[1], scale=0.0625)
         else:
             vts(T.mh[:, 512 + i:640:4], bank(i, 32), 0.0, 0.0625, Op.max, Op.mult, k[0], k[1])
-    if s > 0:
-        act(T.prior[:], T.crow[:, 0:128].indirect(T.gwu[:, 0:10]), Act.Copy, ("crow", "gwu"), ("prior",))
     quant("hm", 0, 128, T.mh[:, 128:640], ("mhz", "hmt0", "hmt1", "hmt2", "hmt3"))
     hat = 192 + A * s
-    bcast(T.hmq[:, 96:128].bitcast(u8), T.hwq[:, hat:hat + A].bitcast(u8), "hm", "lb", ("hmq",))
-    bcast(T.hmp[:, 96:128], T.hwp[:, hat:hat + A], "hm", "lb", ("hmp",))
-    lastw["hwq"] = lastw["hwp"] = [("hm", 96)]
+    bcast(T.hmq[:, 96:128].bitcast(u8), T.hwq[:, hat:hat + A].bitcast(u8), "hm", "lb", ("hmq",), {"hwq": ("hm", 96)})
+    bcast(T.hmp[:, 96:128], T.hwp[:, hat:hat + A], "hm", "lb", ("hmp",), {"hwp": ("hm", 96)})
     pickp("hw", hat, hat + A, "hm", 96, 128, T.colu[:, 0:2], ("hmp", "colu"), ("hwpm",))
+    pickq("hw", hat, hat + A, "hm", 96, 128, T.colu[:, 0:2], ("hmq", "colu"), ("hwqm",))
 
-    quant("hw", 0, 192, T.hot[:], ("hot0", "hot1", "hot2", "hot3"), ("hwqo", "hwpo"))
+    vcp(T.gwu[:], bank(5, 116, 126), ("b5",), ("gwu",))
+    vtt(T.dw[:], bank(5, 116, 126), T.colm[:, 2:12], Op.subtract, ("b5", "colm"), ("dw",))
     if s > 0:
+        run(None, None, (), ("lc",), arr={"lc": ("ct", 4 * s)})
+        src, key = T.lc[:, 0:8], "lc"
+        for r in range(1, s):
+            vtt(T.ctot[:], src, T.lc[:, 8 * r:8 * r + 8], Op.add, ("lc", key), ("ctot",))
+            src, key = T.ctot[:], "ctot"
+        vcp(T.cu[:], src, (key,), ("cu",))
+        act(T.crow[:], T.rowb[:, 0:128].indirect(T.cu[:, 0:8]), Act.Copy, ("rowb", "cu"), ("crow",))
+        act(T.prior[:], T.crow[:, 0:128].indirect(T.gwu[:, 0:10]), Act.Copy, ("crow", "gwu"), ("prior",))
         vtt(T.adm[:], T.prior[:], bank(4, 160), Op.is_lt, ("prior", "b4"), ("adm",))
     else:
         vts(T.adm[:], bank(4, 160), 0.0, None, Op.is_gt, rd=("b4",), wr=("adm",))
@@ -478,24 +439,60 @@ def rank_program(g, core, T, topo):
     vtt(T.fin[:, 0:2], T.fm[:], T.colw[:, 0:2], Op.add, ("fm", "colw"), ("fin0",))
     vtt(T.admt[:], T.scn[:, 15:160:16], T.dw[:], Op.mult, ("scn", "dw"), ("admt",))
     vtt(T.fin[:, 2:12], T.admt[:], T.colw[:, 2:12], Op.add, ("admt", "colw"), ("fin1",))
-    pickq("hw", hat, hat + A, "hm", 96, 128, T.colu[:, 0:2], ("hmq", "colu"), ("hwqm",))
     vcp(T.finu[:], T.fin[:], ("fin0", "fin1"), ("finu",))
-    quant("v", 0, 128, T.vt[:], ("vt",))
+    act(T.mgr[:, 32:192], T.mgt[:, 0:320].indirect(T.finu[:, 2:12]), Act.Copy, ("mgta", "mgtb", "finu"), ("mgr1",))
+    sync(T.mg[0:1, 0:192], T.mgr[0:1, 0:192], "dout", ("mgr0", "mgr1"), name="mg")
 
     def hh(c):
-        return ("hw" + c, "hw" + c + "m", "hw" + c + "o", "finu")
-    for i, (a, b) in enumerate([(0, 128), (128, 192)]):
-        pickq("fo", a, b, "hw", 0, 320, T.finu[:, a // 16:b // 16], hh("q"), ("foq%d" % i,))
-        pickp("fo", a, b, "hw", 0, 320, T.finu[:, a // 16:b // 16], hh("p"), ("fop%d" % i,))
-    sync(T.oc[:, 0:768], T.foq[:, 0:192].bitcast(u8), "dout", ("foq0", "foq1"))
+        return ("hwq", "hwp", "hw" + c + "m", "hw" + c + "o", "finu")
+    mm(7, 128, "v", 0, "hw", 192, rd=("hwq", "hwp", "hwqm", "hwpm"))
+    pickq("fo", 0, 192, "hw", 0, 320, T.finu[:, 0:12], hh("q"), ("foq",))
+    pickp("fo", 0, 192, "hw", 0, 320, T.finu[:, 0:12], hh("p"), ("fop",))
+    vcp(T.ya[:, 192:320], bank(7, 128), ("b7",), ("ya1",))
+    vcp(T.yo[:, 0:96], T.ya[:, 0:320].indirect(T.finu[:, 0:6]), ("ya0", "ya1", "finu"), ("yo0",))
+    act(T.yo[:, 96:192], T.ya[:, 0:320].indirect(T.finu[:, 6:12]), Act.Copy, ("ya0", "ya1", "finu"), ("yo1",))
+    sync(T.oc[:, 0:768], T.foq[:, 0:192].bitcast(u8), "dout", ("foq",), name="oc")
     for k in range(4):
-        sync(T.osc[4 * k:4 * k + 4, 0:192], T.fop[32 * k:32 * k + 4, 0:192], "dout", ("fop0", "fop1"))
-    mm(6, 128, "v", 0, "fo", 0, rd=("foq0", "fop0"))
-    mm(7, 128, "v", 0, "fo", 64, rd=("foq0", "fop0", "foq1", "fop1"))
-    act(T.mgr[:, 32:192], T.mgt[:, 0:320].indirect(T.finu[:, 2:12]), Act.Copy, ("mgta", "mgtb", "finu"), ("mgr1",))
-    run("s", lambda: S.dma_start(T.mg[0:1, 0:192], T.mgr[0:1, 0:192]), ("mgr0", "mgr1"), (), sem="dout")
-    vcp(T.yo[:, 0:128], bank(6, 128), ("b6",), ("yo0",))
-    sync(T.y[:, 0:128], T.yo[:, 0:128], "dout", ("yo0",))
-    vcp(T.yo[:, 128:192], bank(7, 64, 128), ("b7",), ("yo1",))
-    sync(T.y[:, 128:192], T.yo[:, 128:192], "dout", ("yo1",))
+        sync(T.osc[4 * k:4 * k + 4, 0:192], T.fop[32 * k:32 * k + 4, 0:192], "dout", ("fop",), name="osc")
+    sync(T.y[:, 0:192], T.yo[:, 0:192], "dout", ("yo0", "yo1"), name="y")
+
+    place = {n: i for i, n in enumerate(ORDER)}
+    ops.sort(key=lambda op: place.get(op[0], len(place)))
+    waited, lastw, readers, total = {q: {} for q in Q}, {}, {}, {}
+
+    def wait(q, toks):
+        need = {}
+        for n, val in toks:
+            need[n] = max(need.get(n, 0), val)
+        for n in sorted(need):
+            if waited[q].get(n, 0) < need[n]:
+                Q[q].wait_ge(T.sem[n], need[n])
+                waited[q][n] = need[n]
+
+    for _, q, fn, rd, wr, sem, free, arr in ops:
+        if arr is not None:
+            if q:
+                wait(q, [t for k in rd for t in lastw[k]])
+                fn()
+            for k in arr:
+                lastw[k] = [arr[k]]
+            continue
+        toks = []
+        for k in rd:
+            toks += lastw[k]
+            if k[0] == "b":
+                toks += [t for t in readers[k] if t[0] != "q" + q]
+        for k in wr:
+            if k not in free:
+                toks += lastw.get(k, []) + readers.get(k, [])
+        wait(q, toks)
+        n, inc = (sem, 16) if sem else ("q" + q, 1)
+        fn().then_inc(T.sem[n], inc)
+        total[n] = total.get(n, 0) + inc
+        tok = (n, total[n])
+        for k in rd:
+            readers.setdefault(k, []).append(tok)
+        for k in wr:
+            lastw[k] = [tok]
+            readers[k] = []
     wait("g", [(n, total[n]) for n in ("qv", "qs", "qt", "qg", "dout")] + [("lb", lsum["lb"])])

from concourse.bass import DstId, RemoteDMATransfer
from concourse.mybir import dt, AluOpType as Op, AxisListType, ActivationFunctionType as Act

A = 32
EPS, TINY = 1.25 * 2.0 ** -24, 2.0 ** -125
F, B16, U16, CODE, PL = "float32", "bfloat16", "uint16", "float8_e4m3fn_x4", "uint8"

SCRATCH = {}


def _sb(dtype, **names):
    for n, w in names.items():
        SCRATCH[n] = ("sbuf", [128, w], dtype)


def _mx(**names):
    for n, w in names.items():
        SCRATCH[n + "q"] = ("sbuf", [128, w], CODE)
        SCRATCH[n + "p"] = ("sbuf", [128, w], PL)


SCRATCH["psum"] = ("psum", [128, 4096], F)
_sb(F, cst=16, kc=16, kcx=32, kx=16, col0=12, colw=12, colm=12, mk=4, th=4, tri32=32, rst=160, mgt=320,
    r0=224, rx=640, a5=2, mrow=224, jnk=256, tiny=64, kab=16, ps=288,
    ss=64, dw=10, crow=128, prior=160, adm=160, scn=160, admt=10, fin=12, fm=2, mgr=192, ya=320, yo=192)
_sb("int32", ui=4)
_sb(B16, rowb=128, r10=10, rsm=138, k16=128, kst=256, et=516, trt=640, s3t=512, zt=664, xt=1152, wt=2048, vt=512,
    cc=320, cj=160, ot=552, stt=512, s2t=512, tmt=688, mh=640, hot=768, hot10=20,
    lst=16, nz=16, csum=8, ll=32, lc=24, lab=32, lu=16, lcm=2, ctot=8)
_sb(U16, colu=12, invu=8, off=4, gwu=10, cu=8, finu=12)
_mx(e=512, tr=160, s3=128, x=416, k=224, w=512, v=128, ob=138, mm=136, st=128, s2=128, m2=128, tm=172,
    sl=96, win=160, m=128, hm=128, hw=320, fo=192)

SEMAPHORES = ["qv", "qs", "qt", "qg", "dxa", "dx", "dw", "dv", "dz1", "dz2", "dz3", "dz4", "dz5", "dz6", "dz7", "dzq", "dzp",
              "an", "so", "li", "ct", "hm", "la", "lb", "dout"]
_TINY = {n: 2 * i for i, n in enumerate(["cn", "gg", "gd", "gq", "gm", "gd16", "gd64", "thz", "thy", "thr"])}
ORDER = """
zt ui0 mk ll ui3 ui1 xzz psz ui2 et kxa kc col0 xza aq c0 rowb k16 c6 xt otC colu et.2 tri32 kpo c8 s31 s30 colw otA
kqo eq2 s32 eq0 xq s33 trA trB to_aq to_ap h10 kpd c7 kxb tr1 kqd b1 c9 kxc otE mk.2 xq2 eq3 eq1 r1 colm tri32.2 b0 rsm
r0 b3 b4 gg1 a50 trB2 r3 tm1 winpz tm0 wt r4 a51 b2 r2 w3 r10 dg0 dg1 trA.2 h10.2 trA.3 h10.3 rsm.2 th trB.2 mgr0 w4
gg0 w2 w1 gq1 gq0 h10.4 w0 ca4 ca2 ca3 ca0 gd1 cn0 cb0 cb1 kab gm1 mgta rst trq rst.2 kst mm1 cn1 mm3 gd0 mm2 gm0 mm0
otA.2 otC.2 otB gd64 otD s23 s21 b0.2 b1.2 obq b2.2 b5 s20 s22 mmq s2q ps0 b6 ps1 kc0 m20 m22 kc1 m23 m21 mhz winqz st0
vt gd16 tm3 thz mgtb b3.2 st1 m2q stq b4.2 b7 thy tm4 wq2 thr1 thr0 b7.2 lst wq3 invu slq tm1.2 nz csum1 b4.3 to_lst
wq1 s3q llo b7.3 csum0 wq0 winqo b6.2 b5.2 lab0 to_slq winpo slp lab1 tm5 tm2 hot2 tm0.2 hot3 hot0 lcm lu off1 to_slp
off0 off2 to_csum0 fm vq kqf kpf b0.3 fin0 b1.3 hot1 b2.3 b2.4 b3.3 ss0 tmq lc ctot ctot.2 b3.4 b4.4 b5.3 mt2 mt0 ss1
mt1 mt3 cu mq gwu crow b2.5 b0.4 b3.5 hmt2 b1.4 dw hwqo hmt3 hmt1 b6.3 hmt0 prior hmq to_hmq ya0 adm hwqm to_hmp hwpm
scn admt fin1 finu mgr1 mg foq b7.4 ya1 oc fop osc.3 osc.2 osc osc.4 yo1 yo0 y
""".split()


def rank_program(g, core, T, topo):
    s = T.rank_of(core)
    if s is None:
        return
    others = [r for r in range(4) if r != s]
    order = others + [s]
    Q = {"v": g.vector, "s": g.scalar, "t": g.tensor, "g": g, "y": g.sync}
    ops, seen = [], {}

    def run(q, fn, rd=(), wr=(), sem=None, free=(), name=None, arr=None):
        n = name or wr[0]
        seen[n] = seen.get(n, 0) + 1
        ops.append((n if seen[n] == 1 else "%s.%d" % (n, seen[n]), q, fn, tuple(rd), tuple(wr), sem, free, arr))

    V, S, P = g.vector, g.scalar, g.tensor

    def vts(out, in0, s1, s2, op0, op1=None, rd=(), wr=()):
        if op1 is None:
            run("v", lambda: V.tensor_scalar(out, in0, s1, None, op0), rd, wr)
        else:
            run("v", lambda: V.tensor_scalar(out, in0, s1, s2, op0, op1), rd, wr)

    def vtt(out, a, b, op, rd=(), wr=()):
        run("v", lambda: V.tensor_tensor(out, a, b, op), rd, wr)

    def vcp(out, in_, rd=(), wr=()):
        run("v", lambda: V.tensor_copy(out, in_), rd, wr)

    def fill(ap, c, *wr):
        run("v", lambda: V.memset(ap, c), (), wr)

    def vred(out, in_, op, rd=(), wr=()):
        run("v", lambda: V.tensor_reduce(out, in_, AxisListType.X, op), rd, wr)

    def vscan(out, d0, d1, init, op0, op1, rd=(), wr=()):
        run("v", lambda: V.tensor_tensor_scan(out, d0, d1, init, op0, op1), rd, wr)

    def vtr(out, in_, rd=(), wr=()):
        run("v", lambda: V.transpose(out, in_), rd, wr)

    def act(out, in_, func, rd=(), wr=(), **kw):
        run("s", lambda: S.activation(out, in_, func, **kw), rd, wr)

    def iota(out, pattern, base, *wr, cm=0):
        run("g", lambda: g.iota(out, pattern, base, cm, allow_small_or_imprecise_dtypes=True), (), wr)

    def select(out, pattern, op, fl, base, cm, *wr):
        run("g", lambda: g.affine_select(out, out, pattern, op, fl, base, cm), wr, wr)

    def sync(out, in_, sem, rd=(), wr=(), name=None):
        run("y", lambda: g.sync.dma_start(out, in_), rd, wr, sem=sem, name=name)

    def quant(n, a, b, src, rd=(), wr=None):
        run("v", lambda: V.quantize_mx(T[n + "q"][:, a:b], T[n + "p"][:, a:b], src), rd, wr or (n + "q", n + "p"))

    def bank(i, a, b=None):
        return T.psum[:, 512 * i:512 * i + a] if b is None else T.psum[:, 512 * i + a:512 * i + b]

    def mm(i, n, ln, la, rn, ra, start=True, stop=True, rd=None, lrd=None):
        b = "b%d" % i
        run("t", lambda: P.matmul_mx(bank(i, n), T[ln + "q"][:, la:la + 128], T[ln + "p"][:, la:la + 128],
                                     T[rn + "q"][:, ra:ra + n], T[rn + "p"][:, ra:ra + n], start, stop),
            (lrd or (ln + "q", ln + "p")) + (rd or (rn + "q", rn + "p")), (b,), free=() if start else (b,))

    def pickq(dn, c, d, sn, lo, hi, off, rd, wr):
        run("v", lambda: V.tensor_copy(T[dn + "q"][:, c:d].bitcast(dt.uint32),
                                       T[sn + "q"][:, lo:hi].bitcast(dt.uint32).indirect(off)), rd, wr)

    def pickp(dn, c, d, sn, lo, hi, off, rd, wr):
        run("s", lambda: S.activation(T[dn + "p"][:, c:d], T[sn + "p"][:, lo:hi].indirect(off), Act.Copy), rd, wr)

    def tn(n, i=None):
        c = _TINY[n]
        return T.tiny[:, c:c + 2] if i is None else T.tiny[:, c + i:c + i + 1]

    def addr(r):
        rid, pid, _ = topo.addr(T.cores[r])
        return DstId(rid=rid, pnc=pid)

    def msk(es):
        return sum(1 << e for e in es)

    lsum = {"la": 0, "lb": 0}

    def bcast(src, dst, sem, local, rd, arr):
        eng = topo.engines(core, T.cores[others[0]])
        tr = [RemoteDMATransfer(dst_ids=[addr(r) for r in others], dma_engine_mask=msk(eng), remote_sem=T.sem[sem],
                                srcs=[src], dsts=[dst] * len(others))]
        lsum[local] += len(eng)
        run("g", lambda: g.remote_dma_fused(tr, local_sem=T.sem[local]), rd, tuple(arr), name="to_" + rd[0], arr=arr)

    def scatter(srcs, dst, dests, sem, local, rd, masks, arr):
        tr = []
        for r, src in zip(dests, srcs):
            eng = topo.engines(core, T.cores[r])
            es = [e for j in masks[(r - s) % 4] for e in eng[4 * j:4 * j + 4]]
            tr.append(RemoteDMATransfer(dst_ids=[addr(r)], dma_engine_mask=msk(es), remote_sem=T.sem[sem], src=src, dst=dst))
            lsum[local] += len(es)
        run("g", lambda: g.remote_dma_fused(tr, local_sem=T.sem[local]), rd, tuple(arr), name="to_" + rd[0], arr=arr)

    u8 = dt.uint8

    def cs(j):
        return T.cst[:, j:j + 1]

    D1, D2 = 64, 600

    def zeros(n):
        return T.zt[:, D1:D1 + n]

    X0 = 96
    sync(T.xt[:, 384:512], T.x[:, 0:128], "dxa", (), ("xza",))
    sync(T.xt[:, 512:1152], T.x[:, 128:768], "dx", (), ("xt",))
    run("g", lambda: g.iota(T.ui[:, 0:1], [[0, 1]], 0, 1), (), ("ui0",))
    iota(T.rowb[:], [[1, 128]], 0, "rowb")
    iota(T.col0[:], [[16, 12]], 0, "col0")

    def bits(j, op, c):
        run("v", lambda: V.tensor_scalar(T.ui[:, j:j + 1], T.ui[:, 0:1], c, None, op), ("ui0",), ("ui%d" % j,))

    fill(T.xt[:, 0:384], 0.0, "xzz")
    bits(1, Op.bitwise_and, 15)
    bits(2, Op.bitwise_and, 31)
    bits(3, Op.logical_shift_right, 4)
    fill(zeros(536), 0.0, "zt")
    vcp(T.cst[:, 0:4], T.ui[:], ("ui0", "ui1", "ui2", "ui3"), ("c0", "c1", "c2", "c3"))
    fill(T.ll[:], 0.0, "ll")
    quant("x", 0, 128, T.xt[:, 0:512], ("xza", "xzz", "ll"), ("aq", "ap"))
    at1 = A * s
    bcast(T.xq[:, X0:X0 + A].bitcast(u8), T.kq[:, at1:at1 + A].bitcast(u8), "an", "la", ("aq",), {"kq": ("an", 96)})
    bcast(T.xp[:, X0:X0 + A], T.kp[:, at1:at1 + A], "an", "la", ("ap",), {"kp": ("an", 96), "la": ("la", 32)})
    vts(T.colu[:], T.col0[:], cs(1), None, Op.add, rd=("col0", "c1"), wr=("colu",))
    vts(T.colw[:], T.col0[:], cs(1), None, Op.add, rd=("col0", "c1"), wr=("colw",))
    for c, k in ((at1, "o"), (128, "d")):
        pickq("k", c, c + A, "x", X0, X0 + A, T.colu[:, 0:2], ("aq", "colu"), ("kq" + k,))
        pickp("k", c, c + A, "x", X0, X0 + A, T.colu[:, 0:2], ("ap", "colu"), ("kp" + k,))
    sync(T.trt[:, 0:512], zeros(512), "dz5", ("zt",), ("trA",))
    sync(T.trt[:, 512:640], zeros(128), "dz6", ("zt",), ("trB", "trB2", "tr1"))
    sync(T.ot[:, 0:40], zeros(40), "dz7", ("zt",), ("otC", "otD", "otE"))
    sync(T.ot[:, 40:552], zeros(512), "dz4", ("zt",), ("otA", "otB"))
    sync(T.wt[:, :], T.w[:, :], "dw", ("la",), ("wt",))
    sync(T.winq[:, 0:32].bitcast(u8), T.xq[:, 0:32].bitcast(u8), "dzq", ("aq", "la"), ("winqz",))
    sync(T.winp[:, 0:32], T.xp[:, 0:32], "dzp", ("ap", "la"), ("winpz",))
    sync(T.tmt[:, 0:512], zeros(512), "dz2", ("zt", "la"), ("tm0",))
    sync(T.tmt[:, 512:688], zeros(176), "dz3", ("zt", "la"), ("tm1", "tm2", "tm3", "tm4", "tm5"))
    sync(T.mh[:, 128:512], zeros(384), "dz1", ("zt", "la"), ("mhz",))
    sync(T.vt[:, :], T.v[:, :], "dv", ("la",), ("vt",))

    fill(T.et[:], 0.0, "et")
    vts(T.et[:, 3:515:4], T.rowb[:], cs(0), 0.5, Op.is_equal, Op.mult, ("rowb", "c0"), ("et",))
    quant("x", 128, 288, T.xt[:, 512:1152], ("xt",))
    quant("x", 288, 416, T.xt[:, 512:1024], ("xt",), ("xq2", "xp2"))
    for b in range(4):
        quant("e", 128 * b, 128 * b + 128, T.et[:, 3 - b:515 - b], ("et",), ("eq%d" % b, "ep%d" % b))
    act(T.tri32[:], T.rowb[:, 0:32], Act.Sign, ("rowb", "c2"), ("tri32",), scale=-1.0, bias=cs(2))
    act(T.tri32[:], T.tri32[:], Act.Relu, ("tri32",), ("tri32",), scale=-1.0)
    act(cs(6), cs(3), Act.Copy, ("c3",), ("c6",), scale=16.0, bias=32.0)
    act(cs(7), cs(3), Act.Copy, ("c3",), ("c7",), scale=16.0, bias=64.0)
    act(cs(8), cs(1), Act.Copy, ("c1",), ("c8",), scale=-1.0)
    act(cs(9), cs(3), Act.Copy, ("c3",), ("c9",), scale=-16.0, bias=-32.0)
    act(T.ps[0:96, 144:282], T.zt[0:96, D1:D1 + 138], Act.Copy, ("zt",), ("psz",))
    act(T.rsm[:], zeros(138), Act.Copy, ("zt",), ("rsm",), bias=1.0)
    act(T.trt[:, 2:640:4], zeros(160), Act.Copy, ("zt", "trA"), ("tr1",), bias=1.0)
    iota(T.mk[:, 0:3], [[0, 3]], -1, "mk")
    select(T.mk[:, 0:3], [[32, 3]], Op.is_ge, 0.0, -96, 1, "mk")
    tp = [[-1, 128]]
    select(T.trt[:, 0:512:4], tp, Op.is_ge, -1.0, 0, 1, "trA")
    select(T.trt[:, 0:512:4], tp, Op.not_equal, 32.0, 0, 1, "trA")
    iota(T.trt[:, 512:640:4], [[0, 32]], -1, "trB2")
    iota(T.r10[:], [[0, 2], [1, 5]], 0, "r10")
    select(T.rsm[:, 0:10], [[0, 2], [1, 5]], Op.not_equal, 0.0, -4, 0, "rsm")
    select(T.ot[:, 2:16:4], [[0, 4]], Op.is_ge, -1.0, -17, 1, "otE")
    for a, b in ((0, s), (s, 3), (3, 4)):
        if b > a:
            iota(T.kx[:, 4 * a:4 * b], [[1, b - a], [100, 2], [-100, 2]], order[a], "kx" + "abc"[(a > 0) + (a == 3)])
    kxs = ("kxa", "kxb", "kxc") if 0 < s < 3 else ("kxa", "kxc")
    iota(T.k16[:], [[0, 8], [1, 16]], 0, "k16")
    iota(T.kst[:], [[0, 8], [1, 16], [16, 2]], 1, "kst")
    iota(T.kc[:], [[128, 4], [-1, 2], [64, 2]], 32, "kc")
    iota(T.hot10[:], [[0, 20]], 1, "h10")
    select(T.hot10[:], [[32, 2], [-16, 10]], Op.is_ge, 0.0, 0, 1, "h10")
    select(T.hot10[:], [[-32, 2], [16, 10]], Op.is_ge, 0.0, 15, -1, "h10")
    select(T.hot10[:, 10:20], [[0, 10]], Op.is_ge, 0.0, -96, 1, "h10")
    for t in range(4):
        vts(T.s3t[:, t:512:4], T.k16[:], cs(1), None, Op.is_equal, rd=("k16", "c1"), wr=("s3%d" % t,))
    quant("s3", 0, 128, T.s3t[:], ("s30", "s31", "s32", "s33"))
    vcp(T.trt[96:128, 513:640:4], T.trt[96:128, 384:512:4], ("trA",), ("trB",))
    quant("tr", 0, 160, T.trt[:], ("trA", "trB", "trB2", "tr1"))

    kk = ("kq", "kp", "kqo", "kpo", "kqd", "kpd")
    run_max = [T.r0] + [T.rx] * 4
    o = [0, 0, 160, 320, 480]
    best = [T.r0[:, 159:160], T.rx[:, 159:160]]
    for j in (0, 1, 4, 3, 2):
        mm(j, 160, "x", 128 + 32 * j, "k", 0, rd=kk, lrd=("xq", "xp", "xq2", "xp2") if j > 1 else None)
    for j in (0, 1, 4, 3, 2):
        vscan(run_max[j][:, o[j]:o[j] + 160], bank(j, 160), zeros(160), -1e29, Op.max, Op.add, ("b%d" % j, "zt"), ("r%d" % j,))

    def below(i, dst, a, step):
        end = 128 - (step > 1)
        n = len(range(a, end, step))
        act(T.jnk[:, 128 * i:128 * i + n], run_max[i][:, a:end:step], Act.Sign, ("r%d" % i,),
            (dst + str(i), "jnk%d" % i), scale=-1.0, bias=best[i], accum_out=tn(dst, i))

    for i in range(2):
        a5 = T.a5[:, i:i + 1]
        act(a5, best[i], Act.Abs, ("r%d" % i,), ("a5%d" % i,), scale=EPS, bias=TINY)
        act(T.r0[:, 192 - 32 * i:224 - 32 * i], T.tri32[:], Act.Identity, ("tri32", "r%d" % i, "a5%d" % i), ("dg%d" % i,),
            scale=a5, bias=best[i])
    act(T.th[:, 0:3], T.mk[:, 0:3], Act.Identity, ("mk", "r0", "a50"), ("th",), scale=T.a5[:, 0:1], bias=best[0])
    for i in range(2):
        below(i, "gg", 0, 1)
        below(i, "gq", 31, 32)
        below(i, "gd", 15, 16)
    for b in range(4):
        mm(b, 128, "e", 128 * b, "x", 0, True, False, rd=("aq", "ap"), lrd=("eq%d" % b, "ep%d" % b))
    vtr(T.mrow[:, 192:224], T.rx[:, 128:160], ("r1",), ("w1",))
    for j in (4, 3):
        vtr(T.mrow[:, 32 * j - 64:32 * j - 32], T.rx[:, o[j] + 128:o[j] + 160], ("r%d" % j,), ("w%d" % j,))
    vtr(T.mrow[:, 96:192], T.r0[:, 128:224], ("r0", "dg0", "dg1"), ("w0",))
    vtr(T.mrow[:, 0:32], T.rx[:, o[2] + 128:o[2] + 160], ("r2",), ("w2",))
    U = 1.0 / 64
    vts(T.cc[:, 96:160], T.mrow[:, 160:224], best[0], U, Op.is_gt, Op.mult, ("w0", "w1", "r0"), ("ca0",))
    for j in (4, 3, 2):
        c = slice(32 * j - 64, 32 * j - 32)
        vts(T.cc[:, c], T.mrow[:, c], T.th[:, j - 2:j - 1], U, Op.is_gt, Op.mult, ("w%d" % j, "th"), ("ca%d" % j,))
    vts(T.cc[:, 288:320], T.mrow[:, 128:160], best[1], U, Op.is_gt, Op.mult, ("w0", "r1"), ("cb0",))
    vts(T.cc[:, 160:288], T.mrow[:, 0:128], best[1], U, Op.is_ge, Op.mult, ("w0", "w2", "w3", "w4", "r1"), ("cb1",))
    act(T.cj[:], T.cc[:, 0:160], Act.Copy, ("ca0", "ca2", "ca3", "ca4"), ("cn0",), accum_out=tn("cn", 0))
    vred(tn("cn", 1), T.cc[:, 160:320], Op.add, ("cb0", "cb1"), ("cn1",))

    def mzb(k, c):
        vts(T.zt[:, 16 * k - 15:16 * k + 16:2], T.kx[:], tn("gq", 1), cs(c), Op.is_equal, Op.mult,
            kxs + ("gq1", "c%d" % c), ("mm%d" % k,))

    act(T.kab[:], T.kx[:], Act.Abs, kxs + ("gq0",), ("kab",), scale=-1.0, bias=tn("gq", 0))
    act(T.zt[:, 0:32:2], T.kab[:], Act.Relu, ("kab", "c1", "c8"), ("mm0",), scale=cs(8), bias=cs(1))
    act(T.zt[:, 32:64:2], T.kab[:], Act.Relu, ("kab", "c6", "c9"), ("mm2",), scale=cs(9), bias=cs(6))
    mzb(1, 1)
    mzb(3, 7)
    quant("mm", 0, 136, T.zt[:, 0:544], ("mm0", "mm1", "mm2", "mm3", "zt"))
    act(tn("gd64"), tn("gd"), Act.Copy, ("gd0", "gd1"), ("gd64",), scale=-64.0)
    for i in range(2):
        act(tn("gm", i), tn("gd", i), Act.Identity, ("gd%d" % i, "gg%d" % i), ("gm%d" % i,), scale=-16.0, bias=tn("gg", i))
        act(T.kcx[:, 16 * i:16 * i + 16], T.kc[:], Act.Identity, ("kc", "gd64"), ("kc%d" % i,), bias=tn("gd64", i))
    at = 32 * (4 - s)
    for i in range(2):
        vts(T.s2t[:, i:512:4], T.k16[:], tn("gm", i), None, Op.is_equal, rd=("k16", "gm%d" % i), wr=("s2%d" % i,))
        vts(T.s2t[:, 2 + i:512:4], T.k16[:], tn("gm", i), at + 16.0, Op.is_equal, Op.mult, ("k16", "gm%d" % i), ("s2%d" % (2 + i),))
    quant("s2", 0, 128, T.s2t[:], ("s20", "s21", "s22", "s23"))

    for i in range(2):
        vts(T.ot[:, 40 + i:552:4], T.rowb[:], tn("gg", i), tn("cn", i), Op.is_equal, Op.is_gt,
            ("rowb", "gg%d" % i, "cn%d" % i), ("ot" + "AB"[i],))
        vts(T.ot[:, i:40:4], T.r10[:], tn("gq", i), tn("cn", i), Op.is_equal, Op.is_gt,
            ("r10", "gq%d" % i, "cn%d" % i), ("ot" + "CD"[i],))
    quant("ob", 0, 138, T.ot[:], ("otA", "otB", "otC", "otD", "otE"))
    mm(5, 138, "tr", 0, "ob", 0)
    mm(6, 138, "tr", 32, "ob", 0)
    vscan(T.ps[:, 0:138], bank(5, 138), T.rsm[:], -17.0, Op.max, Op.mult, ("b5", "rsm"), ("ps0",))
    vscan(T.ps[96:128, 144:282], T.psum[96:128, 6 * 512:6 * 512 + 138], T.rsm[96:128, :], -17.0, Op.max, Op.mult,
          ("b6", "rsm"), ("ps1",))
    pk = (("ps0",), ("ps1", "psz"))

    def pc(i, c):
        return T.ps[:, 144 * i + c:144 * i + c + 1]

    for i in range(2):
        kc = T.kcx[:, 16 * i:16 * i + 16]
        vts(T.zt[:, D2 + 2 + i:D2 + 64:4], kc, pc(i, 137), pc(i, 8), Op.is_equal, Op.min, pk[i] + ("kc%d" % i,), ("m2%d" % (2 + i),))
        vts(T.zt[:, D2 + i:D2 + 64:4], kc, pc(i, 137), pc(i, 3), Op.is_equal, Op.mult, pk[i] + ("kc%d" % i,), ("m2%d" % i,))
    quant("m2", 0, 128, T.zt[:, D2 + 64 - 512:D2 + 64], ("zt", "m20", "m21", "m22", "m23"))
    mm(4, 128, "s2", 0, "m2", 0)
    for i in range(2):
        vts(T.stt[:, i:512:2], T.kst[:], pc(i, 8), None, Op.is_equal, rd=pk[i] + ("kst",), wr=("st%d" % i,))
    quant("st", 0, 128, T.stt[:], ("st0", "st1"))
    vts(T.lst[:], bank(4, 112, 128), 0.0, None, Op.max, rd=("b4",), wr=("lst",))
    mm(7, 128, "st", 0, "mm", 0, True, False)
    mm(7, 128, "st", 0, "mm", 8, False, True)
    vcp(T.invu[:], bank(7, 8), ("b7",), ("invu",))
    pickq("sl", 0, 96, "x", X0, X0 + 192, T.invu[:, 0:6], ("xq", "aq", "invu"), ("slq",))
    pickp("sl", 0, 96, "x", X0, X0 + 192, T.invu[:, 0:6], ("xp", "ap", "invu"), ("slp",))
    scatter([T.lst[:, 4 * r:4 * r + 4] for r in others], T.ll[:, 8 * s:8 * s + 4], others, "li", "lb", ("lst",),
            {1: (0, 1), 2: (2,), 3: (3,)}, {"lli": ("li", 16)})
    scatter([T.slq[:, 32 * i:32 * i + 32].bitcast(u8) for i in range(3)], T.winq[:, at:at + 32].bitcast(u8), others,
            "so", "lb", ("slq",), {1: (2, 3), 2: (0,), 3: (1,)}, {"winq": ("so", 32)})
    scatter([T.slp[:, 32 * i:32 * i + 32] for i in range(3)], T.winp[:, at:at + 32], others, "so", "lb", ("slp",),
            {1: (0, 1), 2: (2,), 3: (3,)}, {"winp": ("so", 32)})
    p2 = ("ps0", "ps1", "psz")
    if s < 3:
        act(T.nz[:], T.lst[:], Act.Sign, ("lst",), ("nz",))
    pickp("win", at, at + 32, "x", X0, X0 + 192, T.invu[:, 6:8], ("xp", "ap", "invu"), ("winpo",))
    act(tn("thy"), T.ps[:, 8:153:144], Act.Sign, p2, ("thy",))
    act(tn("thz"), T.ps[:, 137:282:144], Act.Relu, p2, ("thz",), scale=2.0, bias=-60.0)
    act(tn("gd16"), tn("gd"), Act.Copy, ("gd0", "gd1"), ("gd16",), scale=16.0)
    for i in range(2):
        act(tn("thr", i), tn("thz", i), Act.Copy, ("thz", "thy"), ("thr%d" % i,), scale=tn("thy", i))
    for i in range(2):
        hj = T.hot10[:, 10 * i:10 * i + 10]
        act(T.tmt[:, 640 + i:680:4], hj, Act.Copy, ("h10", "gm%d" % i), ("tm%d" % (2 + i),), scale=tn("gm", i))
        act(T.tmt[:, 642 + i:680:4], hj, Act.Copy, ("h10", "gd16"), ("tm%d" % (4 + i),), scale=tn("gd16", i))
    act(T.tmt[:, 0:512:4], T.et[:, 3:515:4], Act.Copy, ("et", "thr0"), ("tm0",), scale=tn("thr", 0))
    act(T.tmt[:, 513:640:4], T.et[:, 387:515:4], Act.Copy, ("et", "thr1"), ("tm1",), scale=tn("thr", 1))
    if s < 3:
        for h in range(2):
            vtt(T.csum[:, h:8:2], T.nz[:, h:16:4], T.nz[:, 2 + h:16:4], Op.add, ("nz",), ("csum%d" % h,))
        higher = [r for r in others if r > s]
        scatter([T.csum[:, 0:8]] * len(higher), T.lc[:, 8 * s:8 * s + 8], higher, "ct", "lb", ("csum0", "csum1"),
                {1: (1,), 2: (2,), 3: (3,)}, {})
    HB = (5, 6, 7, 4)
    for i in range(4):
        quant("w", 128 * i, 128 * i + 128, T.wt[:, 512 * i:512 * i + 512], ("wt",), ("wq%d" % i, "wp%d" % i))
        mm(HB[i], 192, "w", 128 * i, "x", X0, rd=("xq", "xp", "aq", "ap"), lrd=("wq%d" % i, "wp%d" % i))
        act(T.hot[:, i:768:4], bank(HB[i], 192), Act.Relu, ("b%d" % HB[i],), ("hot%d" % i,), scale=0.0625)
    vcp(T.ll[:, 8 * s:8 * s + 4], T.lst[:, 4 * s:4 * s + 4], ("lst", "ll"), ("llo",))
    pickq("win", at, at + 32, "x", X0, X0 + 192, T.invu[:, 6:8], ("xq", "aq", "invu"), ("winqo",))
    act(T.colm[:], T.colw[:], Act.Copy, ("colw",), ("colm",), bias=-192.0)
    iota(T.rst[:], [[0, 160]], 1, "rst")
    select(T.rst[:], [[0, 10], [1, 16]], Op.not_equal, 0.0, 0, 0, "rst")
    iota(T.mgt[:, 0:192], [[0, 192]], -1, "mgta")
    iota(T.mgt[:, 192:320], [[192, 4], [1, 32]], 0, "mgtb")
    iota(T.mgr[:, 0:32], [[0, 32]], -1, "mgr0")
    quant("tm", 0, 172, T.tmt[:], tuple("tm%d" % i for i in range(6)))
    mm(5, 128, "s3", 0, "tm", 44)
    mm(4, 160, "s3", 0, "tm", 0)
    quant("hw", 0, 192, T.hot[:], ("hot0", "hot1", "hot2", "hot3"), ("hwqo", "hwpo"))
    quant("v", 0, 128, T.vt[:], ("vt",))
    mm(6, 192, "v", 0, "hw", 0, rd=("hwqo", "hwpo"))
    act(T.ya[:, 0:192], bank(6, 192), Act.Copy, ("b6",), ("ya0",))

    L, X = T.ll, T.lab
    rl = ("ll", "llo", "lli")
    vtt(X[:, 0:32:2], L[:, 0:16], L[:, 16:32], Op.max, rl, ("lab0",))
    vtt(X[:, 1:32:2], L[:, 0:16], L[:, 16:32], Op.min, rl, ("lab1",))
    vtt(T.lu[:], X[:, 0:16], X[:, 16:32], Op.max, ("lab0", "lab1"), ("lu",))
    vtt(T.lcm[:], X[:, 0:4:2], X[:, 16:20:2], Op.min, ("lab0",), ("lcm",))
    vcp(T.off[:, 2:4], T.lu[:, 0:4:2], ("lu",), ("off0",))
    for h in range(2):
        vts(T.off[:, h:h + 1], T.lcm[:, h:h + 1], T.lu[:, 1 + 2 * h:2 + 2 * h], T.lu[:, 4 + 2 * h:5 + 2 * h], Op.max, Op.max,
            ("lcm", "lu"), ("off%d" % (1 + h),))

    def ww(c):
        return ("winq", "winp", "win" + c + "o", "win" + c + "z", "off0", "off1", "off2")
    pickq("k", 160, 224, "win", 0, 160, T.off[:, 0:4], ww("q"), ("kqf",))
    pickp("k", 160, 224, "win", 0, 160, T.off[:, 0:4], ww("p"), ("kpf",))
    for b in range(4):
        ee = ("eq%d" % b, "ep%d" % b)
        mm(b, 128, "e", 128 * b, "k", 96, False, b < 2, rd=kk + ("kqf", "kpf"), lrd=ee)
        if b >= 2:
            mm(b, 128, "e", 128 * b, "k", 64, False, True, rd=kk + ("kqf", "kpf"), lrd=ee)
    for b in range(2):
        act(T.ss[:, 32 * b:32 * b + 32], bank(b, 64, 96), Act.Copy, ("b%d" % b,), ("ss%d" % b,))
    vcp(T.mh[:, 2:128:4], bank(2, 96, 128), ("b2",), ("mt2",))
    for b in range(2):
        vtt(T.mh[:, b:128:4], T.ss[:, 32 * b:32 * b + 32], bank(b, 96, 128), Op.add, ("ss%d" % b, "b%d" % b), ("mt%d" % b,))
    vcp(T.mh[:, 3:128:4], bank(3, 96, 128), ("b3",), ("mt3",))
    quant("m", 0, 128, T.mh[:, 0:512], ("mt0", "mt1", "mt2", "mt3", "mhz"))
    for i in range(4):
        mm(i, 128, "w", 128 * i, "m", 0, lrd=("wq%d" % i, "wp%d" % i))
    for i in range(4):
        k = ("b%d" % i,), ("hmt%d" % i,)
        if i % 2 == 0:
            act(T.mh[:, 512 + i:640:4], bank(i, 32), Act.Relu, k[0], k[1], scale=0.0625)
        else:
            vts(T.mh[:, 512 + i:640:4], bank(i, 32), 0.0, 0.0625, Op.max, Op.mult, k[0], k[1])
    quant("hm", 0, 128, T.mh[:, 128:640], ("mhz", "hmt0", "hmt1", "hmt2", "hmt3"))
    hat = 192 + A * s
    bcast(T.hmq[:, 96:128].bitcast(u8), T.hwq[:, hat:hat + A].bitcast(u8), "hm", "lb", ("hmq",), {"hwq": ("hm", 96)})
    bcast(T.hmp[:, 96:128], T.hwp[:, hat:hat + A], "hm", "lb", ("hmp",), {"hwp": ("hm", 96)})
    pickp("hw", hat, hat + A, "hm", 96, 128, T.colu[:, 0:2], ("hmp", "colu"), ("hwpm",))
    pickq("hw", hat, hat + A, "hm", 96, 128, T.colu[:, 0:2], ("hmq", "colu"), ("hwqm",))

    vcp(T.gwu[:], bank(5, 116, 126), ("b5",), ("gwu",))
    vtt(T.dw[:], bank(5, 116, 126), T.colm[:, 2:12], Op.subtract, ("b5", "colm"), ("dw",))
    if s > 0:
        run(None, None, (), ("lc",), arr={"lc": ("ct", 4 * s)})
        src, key = T.lc[:, 0:8], "lc"
        for r in range(1, s):
            vtt(T.ctot[:], src, T.lc[:, 8 * r:8 * r + 8], Op.add, ("lc", key), ("ctot",))
            src, key = T.ctot[:], "ctot"
        vcp(T.cu[:], src, (key,), ("cu",))
        act(T.crow[:], T.rowb[:, 0:128].indirect(T.cu[:, 0:8]), Act.Copy, ("rowb", "cu"), ("crow",))
        act(T.prior[:], T.crow[:, 0:128].indirect(T.gwu[:, 0:10]), Act.Copy, ("crow", "gwu"), ("prior",))
        vtt(T.adm[:], T.prior[:], bank(4, 160), Op.is_lt, ("prior", "b4"), ("adm",))
    else:
        vts(T.adm[:], bank(4, 160), 0.0, None, Op.is_gt, rd=("b4",), wr=("adm",))
    vts(T.fm[:], T.lu[:, 0:4:2], 0.0, 192.0 + A * s, Op.is_gt, Op.mult, ("lu",), ("fm",))
    vscan(T.scn[:], T.rst[:], T.adm[:], 0.0, Op.mult, Op.add, ("rst", "adm"), ("scn",))
    vtt(T.fin[:, 0:2], T.fm[:], T.colw[:, 0:2], Op.add, ("fm", "colw"), ("fin0",))
    vtt(T.admt[:], T.scn[:, 15:160:16], T.dw[:], Op.mult, ("scn", "dw"), ("admt",))
    vtt(T.fin[:, 2:12], T.admt[:], T.colw[:, 2:12], Op.add, ("admt", "colw"), ("fin1",))
    vcp(T.finu[:], T.fin[:], ("fin0", "fin1"), ("finu",))
    act(T.mgr[:, 32:192], T.mgt[:, 0:320].indirect(T.finu[:, 2:12]), Act.Copy, ("mgta", "mgtb", "finu"), ("mgr1",))
    sync(T.mg[0:1, 0:192], T.mgr[0:1, 0:192], "dout", ("mgr0", "mgr1"), name="mg")

    def hh(c):
        return ("hwq", "hwp", "hw" + c + "m", "hw" + c + "o", "finu")
    mm(7, 128, "v", 0, "hw", 192, rd=("hwq", "hwp", "hwqm", "hwpm"))
    pickq("fo", 0, 192, "hw", 0, 320, T.finu[:, 0:12], hh("q"), ("foq",))
    pickp("fo", 0, 192, "hw", 0, 320, T.finu[:, 0:12], hh("p"), ("fop",))
    vcp(T.ya[:, 192:320], bank(7, 128), ("b7",), ("ya1",))
    vcp(T.yo[:, 0:96], T.ya[:, 0:320].indirect(T.finu[:, 0:6]), ("ya0", "ya1", "finu"), ("yo0",))
    act(T.yo[:, 96:192], T.ya[:, 0:320].indirect(T.finu[:, 6:12]), Act.Copy, ("ya0", "ya1", "finu"), ("yo1",))
    sync(T.oc[:, 0:768], T.foq[:, 0:192].bitcast(u8), "dout", ("foq",), name="oc")
    for k in range(4):
        sync(T.osc[4 * k:4 * k + 4, 0:192], T.fop[32 * k:32 * k + 4, 0:192], "dout", ("fop",), name="osc")
    sync(T.y[:, 0:192], T.yo[:, 0:192], "dout", ("yo0", "yo1"), name="y")

    place = {n: i for i, n in enumerate(ORDER)}
    ops.sort(key=lambda op: place.get(op[0], len(place)))
    waited, lastw, readers, total = {q: {} for q in Q}, {}, {}, {}

    def wait(q, toks):
        need = {}
        for n, val in toks:
            need[n] = max(need.get(n, 0), val)
        for n in sorted(need):
            if waited[q].get(n, 0) < need[n]:
                Q[q].wait_ge(T.sem[n], need[n])
                waited[q][n] = need[n]

    for _, q, fn, rd, wr, sem, free, arr in ops:
        if arr is not None:
            if q:
                wait(q, [t for k in rd for t in lastw[k]])
                fn()
            for k in arr:
                lastw[k] = [arr[k]]
            continue
        toks = []
        for k in rd:
            toks += lastw[k]
            if k[0] == "b":
                toks += [t for t in readers[k] if t[0] != "q" + q]
        for k in wr:
            if k not in free:
                toks += lastw.get(k, []) + readers.get(k, [])
        wait(q, toks)
        n, inc = (sem, 16) if sem else ("q" + q, 1)
        fn().then_inc(T.sem[n], inc)
        total[n] = total.get(n, 0) + inc
        tok = (n, total[n])
        for k in rd:
            readers.setdefault(k, []).append(tok)
        for k in wr:
            lastw[k] = [tok]
            readers[k] = []
    wait("g", [(n, total[n]) for n in ("qv", "qs", "qt", "qg", "dout")] + [("lb", lsum["lb"])])
